import numpy as np, ml_dtypes
CORES = [16,17,18,19,32,33,34,35]
N = 8
import mx_ref
BF = ml_dtypes.bfloat16
def gentries(a):
    return np.ascontiguousarray(a.reshape(8, 16, -1).transpose(0, 2, 1)).reshape(8, -1)
def gtable(e):
    e = np.asarray(e); return np.ascontiguousarray(e.reshape(8, -1, 16).transpose(0, 2, 1)).reshape(128, -1).astype(np.int32)
def gcols(t, e):
    v = np.concatenate([t.reshape(8, 16, -1, 4), np.zeros((8, 16, 1, 4), BF)], axis=2)
    return np.ascontiguousarray(np.stack([v[g][:, e[g]] for g in range(8)])).reshape(128, -1)
def tile(rs):
    return np.stack(rs, axis=2).reshape(128, -1).astype(BF)
def cut(t, i, w=512):
    return t[:, w * i:w * i + w]
def pick(q, e):
    c = np.concatenate([q[0].reshape(128, -1, 4), np.zeros((128, 1, 4), np.uint8)], axis=1); s = np.concatenate([q[1], np.ones((16, 1), np.uint8)], axis=1)
    return (np.ascontiguousarray(c[:, e].reshape(128, -1)), np.ascontiguousarray(s[:, e]))
def join(*qs):
    return (np.concatenate([q[0] for q in qs], axis=1), np.concatenate([q[1] for q in qs], axis=1))
def put(q, e, v):
    c, s = q[0].reshape(128, -1, 4).copy(), q[1].copy(); c[:, e] = v[0].reshape(128, -1, 4); s[:, e] = v[1]
    return (c.reshape(128, -1), s)
def pk(c, s):
    return (np.ascontiguousarray(c), mx_ref.live(s))
def emit(q):
    return q[0], q[1]
def packed(v, rng):
    q = [mx_ref.quantize(np.ascontiguousarray(v[r])) for r in range(N)]
    return np.stack([a for a, b in q]), np.stack([mx_ref.plane(b, rng) for a, b in q])
def values_of_codes():
    e, c = np.zeros((128, 128, 4), np.float32), np.zeros((128, 2, 4), np.uint8)
    e[np.arange(128), np.arange(128), 0] = 1
    c[:127, :, 0] = np.arange(256).reshape(2, 128).T[:127]
    return mx_ref.matmul(mx_ref.quantize(e.reshape(128, 512).astype(BF)), (c.reshape(128, 8), np.full((16, 2), 127, np.uint8))).T.reshape(-1).astype(np.float64)
CODE_VALUE, SCALE_VALUE = values_of_codes(), 2.0 ** (np.arange(256) - 127.0)
def decode(q):
    return (CODE_VALUE[q[0]].reshape(16, 8, -1, 4) * SCALE_VALUE[q[1]][:, None, :, None] + 0.0).reshape(128, -1).astype(np.float32)
def f(rng, *shape):
    return mx_ref.flush((rng.standard_normal(shape, dtype=np.float32) * np.exp2(rng.integers(-2, 3, shape[:-1] + (1,)))).astype(BF))
def wide(rng, *shape, cols=0):
    v = rng.standard_normal(shape, dtype=np.float32) * np.exp2(rng.integers(-12, 13, shape)).astype(np.float32)
    if cols: v *= np.repeat(np.exp2(rng.integers(-cols, cols + 1, shape[:-2] + (1, shape[-1] // 4))) * (rng.random(shape[:-2] + (1, shape[-1] // 4)) > 0.0625), 4, axis=-1).astype(np.float32)
    return mx_ref.flush(v.astype(BF))
C, P, H, R = 320, 32, 40, 3
STEP = [1, 2, 4]
def play(s, n):
    place = np.arange(C)
    pile = np.repeat(np.arange(len(n)), n)
    o = np.lexsort((place, -s, pile))
    top = o[np.searchsorted(pile, np.arange(len(n)))]
    rest = np.delete(place, top)
    o = rest[np.lexsort((rest, s[rest], pile[rest]))]
    low = o[np.searchsorted(pile[rest], np.flatnonzero(n >= 2))]
    a, b = top[np.lexsort((top, -s[top]))], low[np.lexsort((low, s[low]))]
    left = np.delete(place, np.concatenate([top, low]))
    m = np.concatenate([np.maximum(n - 2, 0), [len(a), len(b)]])
    came = np.concatenate([left, C + np.arange(len(a)), C + H + np.arange(len(b))])
    k = np.repeat(np.arange(len(m)), m)
    e = came[np.lexsort((np.arange(C), k, -m[k]))]
    m = m[np.argsort(-m, kind="stable")]
    return a, b, e, m[m > 0]
def big(v):
    v = v.astype(np.float32)
    v[np.abs(v) < np.float32(2.0 ** -16)] = 0
    return v.astype(BF)
def sizes(rng, n, c, *shape):
    e = np.argsort(rng.random(shape + (c - 1,)), axis=-1)[..., :n - 1] + 1
    return np.diff(np.sort(e, axis=-1), axis=-1, prepend=0, append=c)
def pilelist(n):
    return np.stack([gtable(n[r]) for r in range(N)])
def numbers_of(rng):
    return {"x": big(f(rng, N, 128, 4 * C)), "u": np.array(f(rng, N, 128, 512)), "v": np.array(f(rng, N, 128, 512))}
def layers(rng):
    return big(f(rng, N, 128, 2048)).reshape(N, 8, 16, 4, 8, 16, 4)
def weights(rng, w):
    c, p = packed(np.ascontiguousarray(w).reshape(N, 128, 2048), rng)
    return {"wc": c, "ws": p}
def signs(rng):
    return np.stack([rng.permutation(8) % 2 * 2.0 - 1.0 for r in range(N)])
def setup_inputs(rng):
    return {**numbers_of(rng), **weights(rng, layers(rng)), "z": pilelist(sizes(rng, P, C, N, 8))}
def setup_inputs_ties(rng):
    d = numbers_of(rng)
    e = rng.permutation(N)
    x = d["x"].reshape(N, 8, 16, C, 4)
    for r in range(N):
        k = np.zeros(C, int) if r == e[0] else rng.permutation(C) % 3
        a = x[r][:, :8, :3].copy()
        a[:, :, 2] = 0
        x[r][:, :8] = a[:, :, k]
    x[e[1]] = 0
    u = d["u"].reshape(N, 8, 16, 128, 4)
    u[:, :, 8:, ::16] = 0
    w = layers(rng)
    w[:, :, 8:, :, :, :8] = 0
    return {"x": x.reshape(N, 128, 4 * C), "u": u.reshape(N, 128, 512), "v": d["v"], **weights(rng, w), "z": pilelist(sizes(rng, P, C, N, 8))}
def setup_inputs_near(rng):
    d = numbers_of(rng)
    x = np.zeros((N, 8, 16, C, 4), np.float32)
    u = d["u"].reshape(N, 128, 128, 4)
    u[:, :, ::16] = 0
    n = sizes(rng, P, C, N, 8)
    o, c = rng.permutation(N) % 4, signs(rng)
    upper = np.arange(C) // (C // 2)
    for r in range(N):
        i = (np.arange(C) + rng.integers(0, C, (8, 1))) % C
        if o[r] < 2:
            for g in np.flatnonzero(c[r] > 0)[:2]:
                last = int(np.sum(n[r, g, :int(np.argmax(n[r, g])) + 1])) - 1
                i[g] = (last - np.arange(C)) % C
        s = (i + 1) // 2
        size = 1.0 if o[r] < 2 else 2.0 ** -4
        if o[r] < 2: x[r, :, 0, :, 0] = c[r][:, None]
        if o[r] == 3:
            s = i % (C // 2)
            k = rng.permutation(8)
            for g in range(8):
                if k[g] % 2:
                    s[g] = (np.arange(C) - C // 4 - 1) % (C // 2)
                    n[r, g] = 1
                    n[r, g, rng.integers(P)] = C - P + 1
                else: n[r, g] = np.tile(sizes(rng, P // 2, C // 2), 2)
                more = upper ^ (k[g] // 2 % 2)
                x[r, g, 0, :, 0] = more * 4.5 * 2.0 ** -30
                x[r, g, 1, :, 0] = (1 - more) * 4.0 * 2.0 ** -30
        digit = ((s[:, :, None] >> np.arange(8)) & 1) * np.exp2(np.arange(8) - 23.0) * size
        x[r, :, 8] = digit[:, :, :4]
        x[r, :, 9] = digit[:, :, 4:]
        x[r, :, 10:] = rng.integers(4, 8, (8, 6, C, 4)) * 2.0 ** -20 * size
        q = 1.0 if o[r] == 0 else 2.0 ** -30
        for h in range(0, 128, 16):
            u[r, h, h, 0] = q
            u[r, h + 8:h + 10, h] = q
            if o[r] == 3:
                u[r, h, h, 0] = 1.125 * q
                u[r, h + 1, h, 0] = 1.25 * q
    w = layers(rng)
    w[:, :, :10] = 0
    w[:, :, :, :, :, :10] = 0
    return {"x": x.reshape(N, 128, 4 * C).astype(BF), "u": u.reshape(N, 128, 512), "v": d["v"], **weights(rng, w), "z": pilelist(n)}
def setup_inputs_huge(rng):
    d = numbers_of(rng)
    c = np.stack([rng.permutation(C) % 2 * 2.0 - 1.0 for r in range(N)])
    one = rng.permutation(N) < N // 2
    c[one] = -1
    x = (0.6 + 0.2 * rng.random((N, 128, C, 4))) * 2.0 ** 30
    u = d["u"].reshape(N, 128, 128, 4)
    a = 2.0 ** 30 * (1 - 0.25 * rng.random((N, 128, 8, 4)))
    for r in np.flatnonzero(one):
        for k in (x[r], a[r]):
            k[:] = 2.0 ** 30 * (1 - 0.0625 * rng.integers(0, 2, k.shape))
            k[::8, :, 0] = 2.0 ** 30
    x *= c[:, None, :, None]
    a *= signs(rng)[:, None, :, None]
    u[:, :, ::16] = a.astype(np.float32).astype(BF)
    w = np.zeros((N, 128, 4, 128, 4), np.float32)
    i = np.arange(128)
    for b in range(4): w[:, i, b, i, b] = 1
    return {"x": x.astype(np.float32).reshape(N, 128, 4 * C).astype(BF), "u": u.reshape(N, 128, 512), "v": d["v"], **weights(rng, w.astype(BF)), "z": pilelist(sizes(rng, P, C, N, 8))}
def oddsizes(rng, k):
    if k == 0: return 2 * R + sizes(rng, P, C - 2 * R * P)
    if k == 3: return rng.permutation(C // P + (np.arange(P) < C % P))
    if k == 4: return np.sort(sizes(rng, P, C))
    if k == 7: return np.sort(sizes(rng, P, C))[::-1]
    o = np.ones(P, int)
    if k == 8:
        i = np.sort(rng.permutation(P)[:2])
        o[i[0]] = (C - P + 2) // 2 - rng.integers(1, 9)
        o[i[1]] = C - P + 2 - o[i[0]]
        return o
    if k == 2: o += 1
    if k == 5: o += np.arange(P) % 2
    if k == 6: o += 2
    o[0] += C - np.sum(o)
    return rng.permutation(o)
def setup_inputs_ragged(rng):
    d = numbers_of(rng)
    h = int(rng.integers(8))
    n = np.stack([np.stack([oddsizes(rng, 8 if k == 1 and r % 2 else k) for k in np.insert(1 + rng.permutation(7), h, 0)]) for r in range(N)])
    x, u = d["x"].reshape(N, 128, C, 4), d["u"].reshape(N, 128, 128, 4)
    for r in range(0, N, 2):
        g = int(np.argmax(np.max(n[r], axis=1)))
        last = int(np.sum(n[r, g, :int(np.argmax(n[r, g])) + 1])) - 1
        k = big(u[r, :, 16 * g])
        x[r, :, last] = -k if r % 4 else k
    d["x"] = x.reshape(N, 128, 4 * C)
    return {**d, **weights(rng, layers(rng)), "z": pilelist(n)}
def setup_inputs_spread(rng):
    d = setup_inputs(rng)
    d["x"] = big(wide(rng, N, 128, 4 * C, cols=6))
    return d
def check_inputs(d):
    b = []
    for k in ("x", "u", "v"):
        a = np.abs(d[k].astype(np.float32))
        if not (np.isfinite(a).all() and ((a == 0) | (a >= 2.0 ** -30) & (a <= 2.0 ** 30)).all()): b.append("a value of " + k)
    none, least, most = [emit(mx_ref.quantize(np.full((128, 16), k, np.float32).astype(BF)))[1][0, 0] for k in (0.0, 2.0 ** -30, 2.0 ** 30)]
    for r in range(N):
        if ((d["wc"][r] == 0x7F) | (d["wc"][r] == 0xFF)).any(): b.append("wc: a code that is no number")
        s = mx_ref.live(d["ws"][r])
        if ((s != none) & ((s < least) | (s > most))).any(): b.append("ws: a scale out of range")
        n = gentries(d["z"][r]).astype(np.int64)
        if (n < 1).any(): b.append("z: a size under 1")
        if (np.sum(n, axis=1) != C).any(): b.append("z: a sum of sizes")
    return b
def reference(x, u, v, wc, ws, z):
    qu = [mx_ref.quantize(u[r]) for r in range(N)]
    lay = [pk(wc[r], ws[r]) for r in range(N)]
    now = [x[r] for r in range(N)]
    size = [list(gentries(z[r])) for r in range(N)]
    for t in range(R):
        given, sent, new = [], [], []
        for r in range(N):
            s = mx_ref.matmul(qu[r], mx_ref.quantize(now[r]))[::16] + np.float32(0.0)
            e, h = np.full((8, 2 * H), -1), np.zeros((8, C), int)
            for g in range(8):
                a, b, h[g], size[r][g] = play(s[g], size[r][g])
                e[g, :len(a)] = a
                e[g, H:H + len(b)] = b
            k = gcols(now[r], e)
            given.append(k)
            sent.append(mx_ref.quantize(k))
            new.append(h)
        came = decode(join(*sent))
        for r in range(N):
            k = given[r]
            d = cut(came, r ^ STEP[t], 8 * H)
            q = mx_ref.quantize(np.ascontiguousarray(((k.astype(np.float32) + d) * np.float32(0.5)).astype(BF)))
            c = tile([np.maximum(mx_ref.matmul(pick(lay[r], np.arange(128 * b, 128 * b + 128)), q), np.float32(0.0)) * np.float32(0.03125) + k[:, b::4].astype(np.float32) for b in range(4)])
            now[r] = gcols(np.concatenate([now[r], c], axis=1), new[r])
    y, oz = np.zeros((N, 128, C), np.float32), np.zeros((N, 8, H), np.float32)
    oc, osc = np.zeros((N, 128, 4 * C), np.uint8), np.zeros((N, 16, C), np.uint8)
    for r in range(N):
        q = mx_ref.quantize(now[r])
        y[r] = mx_ref.matmul(mx_ref.quantize(v[r]), q)
        for g in range(8): oz[r, g, :len(size[r][g])] = size[r][g]
        oc[r], osc[r] = emit(q)
    return {"y": y, "oz": oz, "oc": oc, "osc": osc}

@@ -1,0 +1,716 @@
+from concourse.mybir import dt, AluOpType, ActivationFunctionType
+
+C = 320
+NJ = [64, 72, 72]
+NB = [4, 5, 5]
+STEP = [1, 2, 4]
+XV = 40
+F32, BF, I32, U16, Q8, U8 = "float32", "bfloat16", "int32", "uint16", "float8_e4m3fn_x4", "uint8"
+BIG = 1e29
+
+SCRATCH = {}
+
+
+def _decl(names, n, d, where="sbuf"):
+    for k in names.split():
+        SCRATCH[k] = (where, [128, n], d)
+
+
+_decl("XW0 XW1", 1608, BF)
+_decl("DW", 1288, BF)
+_decl("ut vt At Mt", 512, BF)
+_decl("Ah", 320, BF)
+_decl("Eb", 516, BF)
+_decl("qx0 qx1 qx2 qx3 ql0 ql1", 320, Q8)
+_decl("sx0 sx1 sx2 sx3 sl0 sl1", 320, U8)
+_decl("ql2", 208, Q8)
+_decl("sl2", 208, U8)
+_decl("qw qe", 512, Q8)
+_decl("sw se", 512, U8)
+_decl("qu qp qv qa qm", 128, Q8)
+_decl("su sp sv sa sm", 128, U8)
+_decl("pA pB pC0 pC1 pC2 pC3", 512, F32, "psum")
+_decl("SP nr cm K4 io4 ym L2 Rr", 320, F32)
+_decl("M Mx PS", 336, F32)
+_decl("WZ", 3200, F32)
+_decl("R0", 768, F32)
+_decl("LA0 LA1 LA2 LB0 LB1", 20, U16)
+_decl("LX tabs tz", 80, U16)
+_decl("zi pI", 2, I32)
+_decl("CI", 8, I32)
+_decl("CF", 32, F32)
+_decl("zb zT", 64, F32)
+_decl("MK KP io", 384, F32)
+_decl("D16 D4 lev ctab nMx st2 val0 erow y2 z2 g80 x80", 80, F32)
+_decl("val T1 T2 T3 vb uu ww src", 96, F32)
+_decl("tb ab fl Fs io3", 208, BF)
+_decl("kk Vr yv Vo", 48, F32)
+_decl("NN va tr jk V0 g2 o2", 192, F32)
+_decl("ES", 384, F32)
+_decl("s80 vm vs", 240, F32)
+_decl("ZM ZO", 288, F32)
+_decl("ZA ZB ZC SR sm5", 128, F32)
+_decl("ow", 256, F32)
+_decl("li lj", 80, I32)
+
+DMAS = ["x", "u", "z", "wc", "ws", "v", "y", "oc", "oz", "os0", "os1", "os2", "os3"]
+SEMAPHORES = ["eV", "eS", "eP", "eG", "sent"] + ["d" + k for k in DMAS] + ["r%d" % k for k in range(8)]
+
+
+def ap(name, lo=0, hi=None, step=1, ind=None, cast=None):
+    if hi is None:
+        hi = SCRATCH[name][1][1]
+    return (name, lo, hi, step, ind, cast)
+
+
+def col(name, c):
+    return ap(name, c, c + 1)
+
+
+def count(a):
+    if a[4] is not None:
+        return 16 * (a[4][2] - a[4][1])
+    return len(range(a[1], a[2], a[3]))
+
+
+def build(near):
+    ops = []
+    AL, AF = AluOpType, ActivationFunctionType
+
+    def two(a):
+        return SCRATCH[a[0]][2] in (BF, U16)
+
+    def rec(q, kind, args, outs, ins, ns, lat=0):
+        rd, wr = [], []
+        for a in ins:
+            if isinstance(a, tuple):
+                (wr if SCRATCH[a[0]][0] == "psum" else rd).append(a)
+                if a[4] is not None:
+                    rd.append(a[4])
+        for a in outs:
+            wr.append(a)
+            if a[4] is not None:
+                rd.append(a[4])
+        ops.append({"q": q, "kind": kind, "args": args, "rd": rd, "wr": wr, "ns": ns, "lat": lat, "up": 0.0})
+        return len(ops) - 1
+
+    def first(v=1500.0):
+        ops[-1]["up"] = v
+
+    def vns(out, a, k=1.0):
+        if out[4] is not None:
+            return 60 + 3.8 * count(out)
+        if a[4] is not None:
+            return 60 + 1.6 * count(a)
+        return max(64, k * count(out)) + 10
+
+    def half(*aps):
+        return 0.5 if all(two(a) for a in aps) else 1.0
+
+    def tt(out, a, b, op):
+        k = 1.0 if "psum" in (SCRATCH[a[0]][0], SCRATCH[b[0]][0]) else 2.0
+        rec("V", "tensor_tensor", (out, a, b, op), [out], [a, b], vns(out, a, k))
+
+    def ts(out, a, s1, op0, s2=None, op1=None):
+        args = (out, a, s1, s2, op0) if op1 is None else (out, a, s1, s2, op0, op1)
+        rec("V", "tensor_scalar", args, [out], [a, s1, s2], vns(out, a, half(out, a)))
+
+    def cp(out, a):
+        rec("V", "tensor_copy", (out, a), [out], [a], vns(out, a, half(out, a)))
+
+    def scan(out, a, b, init, op0, op1):
+        rec("V", "tensor_tensor_scan", (out, a, b, init, op0, op1), [out], [a, b], vns(out, a, half(out, a, b)))
+
+    def mset(out, v):
+        rec("V", "memset", (out, v), [out], [], vns(out, out, half(out)))
+
+    def tr(out, a):
+        rec("V", "transpose", (out, a), [out], [a], vns(out, a))
+
+    def quant(q, s, a):
+        rec("V", "quantize_mx", (q, s, a), [q, s], [a], 20 + 0.27 * count(a))
+
+    def act(out, a, f, bias=None, scale=None, acc=None):
+        n = 80 + (1.6 if a[4] is not None else 1.0) * count(a) + (25 if acc else 0)
+        rec("S", "activation", (out, a, f, bias, scale, acc), [out] + ([acc] if acc else []), [a, bias, scale], n)
+
+    def lin(out, a, scale, bias=None):
+        act(out, a, AF.Identity, bias, scale)
+
+    def mm(out, w, ws, x, xs):
+        rec("P", "matmul_mx", (out, w, ws, x, xs, True, True), [ap(out[0])], [w, ws, x, xs], 20 + 0.7 * count(x))
+
+    def iota(out, pat, base, ch=0):
+        rec("G", "iota", (out, pat, base, ch), [out], [], 130 + 2.0 * count(out))
+
+    def fill(out, v=0):
+        iota(out, [[0, count(out)]], v)
+
+    def dma(q, name, outs, ins, lat=2000):
+        rec(q, "dma", name, outs, ins, 60, lat)
+
+    rn = [0]
+
+    def send(t, src, dst, lat):
+        k = rec("G", "send", (t, src, dst, rn[0]), [], [src], 300)
+        j = rec("R", "recv", (t, rn[0]), [dst], [], 0, lat)
+        ops[j]["after"] = k
+        rn[0] += 1
+
+    dma("S", "z", [ap("zi")], [])
+    first(9000.0)
+    dma("Y", "x", [ap("XW0", 0, 1280)], [], 2600)
+    first(9000.0)
+    dma("S", "u", [ap("ut")], [], 2200)
+    first(9000.0)
+    dma("Y", "wc", [ap("qw")], [], 3500)
+    first(30000.0)
+    dma("Y", "ws", [ap("sw")], [], 3500)
+    first(30000.0)
+    dma("Y", "v", [ap("vt")], [], 3500)
+    first(40000.0)
+
+    P3, SG, H8, P16, P32, H, I8, X4, SIG, NSG, BGB, THR, C16, RZB, QO, SO, I2, N4, MH = range(19)
+    iota(col("pI", 0), [[0, 1]], 0, 1)
+    first()
+    p = col("pI", 0)
+    ts(col("CI", P3), p, 3, AL.bitwise_and)
+    ts(col("CI", SG), p, 2, AL.logical_shift_right, 1, AL.bitwise_and)
+    ts(col("CI", H8), p, 3, AL.logical_shift_right, 1, AL.bitwise_and)
+    ts(col("CI", P16), p, 15, AL.bitwise_and)
+    ts(col("CI", P32), p, 31, AL.bitwise_and)
+    ts(col("CI", H), p, 2, AL.logical_shift_right, 3, AL.bitwise_and)
+    cp(ap("CF", 0, 6), ap("CI", 0, 6))
+
+    def cf(k):
+        return col("CF", k)
+    lin(cf(I8), cf(H8), 4.0, cf(P3))
+    lin(cf(X4), cf(SG), -8.0, cf(P16))
+    lin(cf(SIG), cf(SG), -2.0, 1.0)
+    lin(cf(NSG), cf(SG), -1.0)
+    ts(cf(BGB), cf(SG), -BIG, AL.mult, BIG, AL.add)
+    lin(cf(THR), cf(SG), -1e26, -0.5e26)
+    lin(cf(C16), cf(P3), 1.0, 1600.0)
+    lin(cf(RZB), cf(SG), 64.0, 19.5)
+    lin(cf(QO), cf(SG), -800.0, 800.0)
+    lin(cf(SO), cf(SG), -1600.0, 1600.0)
+    lin(cf(26), cf(SG), 800.0)
+    lin(cf(I2), cf(I8), 2.0, cf(SG))
+    lin(cf(N4), cf(SG), -1.0, 400.0)
+    iota(ap("ctab"), [[16, 80]], 0)
+    iota(ap("io", 0, 96), [[0, 12], [1, 8]], 0)
+    iota(ap("io", 96, 288), [[0, 24], [1, 8]], 0)
+    iota(ap("io", 288, 384), [[0, 6], [1, 16]], 0)
+    for lo, hi, k in ((0, 96, I8), (96, 288, I8), (288, 384, P16)):
+        ts(ap("MK", lo, hi), ap("io", lo, hi), cf(k), AL.is_equal)
+        act(ap("KP", lo, hi), ap("io", lo, hi), AF.Sign)
+
+    def m16(n, k="MK"):
+        return ap(k, 288, 288 + n)
+    lin(ap("D16"), m16(80), cf(SIG))
+    for k in range(2):
+        iota(ap("io4", 160 * k, 160 * k + 160), [[0, 40], [1, 4]], 0)
+        iota(ap("cm", 160 * k, 160 * k + 160), [[1, 160]], 160 * k - 400)
+    ts(ap("D4"), ap("io4", 0, 80), cf(H), AL.is_equal)
+    lin(ap("CF", MH, MH + 4), ap("D4", 0, 4), 4.0)
+    act(ap("K4"), ap("io4"), AF.Sign)
+    iota(ap("io3", 0, 205), [[-8, 5], [1, 41]], 0)
+    ts(ap("Fs", 0, 205), ap("io3", 0, 205), cf(I8), AL.not_equal, 2.0, AL.mult)
+    lin(ap("fl", 0, 205), ap("Fs", 0, 205), 1.0, -1.0)
+    mset(ap("fl", 0, 205, 41), 0.0)
+    UT, ZT, SW, DUP, DUP2 = [ap("tabs", a, b) for a, b in ((0, 8), (8, 10), (10, 16), (16, 21), (22, 27))]
+    RZ, RZ2, ST0 = ap("tabs", 28, 33), ap("tabs", 34, 39), ap("tabs", 52, 56)
+    cp(UT, ap("ctab", 0, 8))
+    ts(ZT, ap("ctab", 0, 4, 2), cf(P32), AL.add)
+    ts(SW, ap("ctab", 0, 6), cf(X4), AL.add, 4.0, AL.add)
+    K6 = ap("sm5", 16, 22)
+    lin(K6, ap("ctab", 0, 6), 0.5, cf(I8))
+    cp(DUP, ap("sm5", 16, 21))
+    lin(col("sm5", 30), cf(SG), 48.0)
+    ts(DUP2, ap("sm5", 16, 21), col("sm5", 30), AL.add)
+    lin(ap("tb", 40, 205, 41), ap("ctab", 0, 5), 1.0, cf(I2))
+    for k in range(2):
+        lin(ap("ow", 200 + 6 * k, 206 + 6 * k), K6, 1.0, 704.0)
+    lin(ap("sm5", 8, 12), ap("ow", 200, 204), cf(SG))
+    lin(ap("T2", 0, 80), ap("ctab"), 1.0, cf(P16))
+    lin(ap("x80"), ap("T2", 0, 80), 1.0, -1600.0)
+    lin(ap("kk"), ap("ctab", 0, 48), 1.0 / 1024)
+    iota(ap("lev"), [[0, 10], [1, 2], [0, 4]], 1)
+    iota(ap("sm5", 32, 38), [[4, 3], [0, 2]], 17)
+    iota(ap("sm5", 40, 45), [[1, 5]], 0)
+    act(ap("vb", 48, 96), ap("kk"), AF.Relu, -31.0, 64.0)
+    act(ap("src", 32, 48), ap("kk", 32, 48), AF.Identity, 322.0 - 40 * 32, 40 * 64.0)
+    lin(ap("V0", 48, 96), ap("kk"), 0.0, -BIG)
+    lin(ap("V0", 144, 192), ap("kk"), 0.0, -BIG)
+    lin(ap("g80"), ap("lev"), -BIG, 1.5 * BIG)
+    for k in range(2):
+        fill(ap("R0", 160 * k, 160 * k + 160))
+        mset(ap("XW%d" % k, 1280, 1608), 0.0)
+    fill(ap("DW", 1280, 1288))
+    for k in ("M", "Mx", "PS"):
+        mset(ap(k, 0, 1), -400.0)
+    fill(ap("val", 64, 96))
+    fill(ap("T3", 80, 96))
+    mset(ap("Mt"), 0.0)
+    first(20000.0)
+    fill(ap("NN", 32, 48))
+    fill(ap("vb", 38, 48))
+    fill(ap("vb", 32, 33), 34)
+    fill(ap("SR", 40, 48))
+    fill(ap("SR", 104, 112))
+    mset(ap("Eb"), 0.5)
+    rec("G", "affine_select", (ap("Eb"), ap("Eb"), [[-1, 516]], AL.is_equal, 0.0, 3, 4), [ap("Eb")], [ap("Eb")], 1200)
+    for b in range(4):
+        quant(ap("qe", 128 * b, 128 * b + 128), ap("se", 128 * b, 128 * b + 128), ap("Eb", 3 - b, 515 - b))
+    for lo in (0, 160, 800, 960, 1600, 1760, 2400, 2560):
+        fill(ap("WZ", lo, lo + 160))
+    if not all(near):
+        mset(ap("At", 256, 512), 0.0)
+        quant(ap("ql2", 80, 208), ap("sl2", 80, 208), ap("Mt"))
+
+    quant(ap("qu"), ap("su"), ap("ut"))
+    cp(ap("qp", cast=dt.uint32), ap("qu", ind=UT, cast=dt.uint32))
+    act(ap("sp"), ap("su", ind=UT), AF.Copy)
+    quant(ap("qv"), ap("sv"), ap("vt"))
+
+    cp(ap("CF", 24, 26), ap("zi"))
+    for b in range(2):
+        lin(ap("zb", 32 * b, 32 * b + 32), ap("ctab", 0, 32), 0.0, cf(24 + b))
+    tr(ap("zT"), ap("zb"))
+    cp(ap("NN", 0, 32), ap("zT", ind=ZT))
+
+    def nn(t, n=48):
+        return ap("NN", 48 * t, 48 * t + n)
+
+    def en(t, n=48):
+        o = 0 if t == 0 else 48 + 48 * t
+        return ap("ES", o, o + n)
+
+    def st(t, n=48):
+        o = 48 if t == 0 else 192 + 48 * t
+        return ap("ES", o, o + n)
+    scan(en(0), nn(0), nn(0), 0.0, AL.add, AL.max)
+    tt(st(0), en(0), nn(0), AL.subtract)
+    tt(ap("ZA", 0, 96), ap("ES", 0, 96), ap("MK", 0, 96), AL.mult)
+    scan(ap("ZB", 0, 96), ap("KP", 0, 96), ap("ZA", 0, 96), 0.0, AL.mult, AL.add)
+    tt(ap("sm5", 48, 52), ap("ZB", 55, 87, 8), ap("sm5", 8, 12), AL.max)
+    cp(ST0, ap("sm5", 48, 52))
+    mset(ap("jk", 0, 64), -BIG)
+    cp(ap("R0", ind=ST0), ap("jk", 0, 64))
+    cp(ap("tz", 0, 6), ap("ZB", 7, 48, 8))
+    tt(ap("g2", 0, 48), en(0), m16(48), AL.mult)
+    scan(ap("o2", 0, 48), m16(48, "KP"), ap("g2", 0, 48), 0.0, AL.mult, AL.add)
+    cp(ap("tz", 20, 23), ap("o2", 15, 48, 16))
+
+    def giving(lo, hi, starts, out):
+        lin(ap("va", lo, hi), ap("NN", lo, hi), 1e26, cf(THR))
+        ts(ap("tr", lo, hi), ap("va", lo, hi), -1.0, AL.mult, 320.0, AL.min)
+        tt(out, ap("tr", lo, hi), starts, AL.max)
+    giving(0, 48, st(0), ap("jk", 64, 112))
+    act(ap("s80", 0, 80), ap("jk", 64, 112, ind=DUP), AF.Identity, -400.0)
+
+    act(ap("vb", 0, 32), nn(0, 32), AF.Copy)
+    for j in range(5):
+        act(ap("ZM", 32 * j, 32 * j + 32), nn(0, 32), AF.Sign, -1.5 - j, None, col("sm5", 56 + j))
+    lin(col("sm5", 62), col("sm5", 56), 0.5, 16.0)
+    ts(ap("sm5", 64, 69), ap("sm5", 40, 45), col("sm5", 62), AL.is_le)
+    lin(ap("sm5", 88, 93), ap("sm5", 56, 61), 0.5)
+    tt(ap("sm5", 96, 101), ap("sm5", 88, 93), ap("sm5", 33, 38), AL.add)
+    tt(ap("vb", 33, 38), ap("sm5", 96, 101), ap("sm5", 64, 69), AL.add)
+    tt(ap("ZC", 64, 104), ap("vb", 0, 40), ap("kk", 0, 40), AL.subtract)
+    tt(ap("ZC", 0, 40), ap("ZC", 64, 104), ap("MK", 0, 40), AL.mult)
+    scan(ap("ZA", 40, 80), ap("KP", 0, 40), ap("ZC", 0, 40), 0.0, AL.mult, AL.add)
+    for m in range(5):
+        act(ap("ZO", 40 * m, 40 * m + 40), ap("ZC", 64, 104), AF.Sign, col("ZA", 47 + 8 * m), -1.0, col("sm5", 104 + m))
+    ts(RZ, ap("sm5", 104, 109), -0.5, AL.mult, cf(RZB), AL.add)
+    ts(RZ2, ap("sm5", 104, 109), -0.5, AL.mult, 19.5, AL.add)
+    act(ap("y2"), ap("vb", ind=DUP2), AF.Copy)
+    cp(ap("SR", ind=RZ), ap("y2"))
+    for t in (1, 2):
+        u = ap("uu", 48 * t - 48, 48 * t)
+        w = ap("ww", 48 * t - 48, 48 * t)
+        act(u, ap("SR", 64, 112), AF.Relu, -2000.0 * t, 1000.0)
+        tt(w, ap("SR", 0, 48), u, AL.subtract)
+        act(nn(t), w, AF.Relu, -2.0 * t)
+    act(nn(3), ap("SR", 0, 48), AF.Relu, -6.0)
+    for t in (1, 2, 3):
+        scan(en(t), nn(t), nn(t), 0.0, AL.add, AL.max)
+    tt(st(1), en(1), nn(1), AL.subtract)
+    tt(ap("ES", 288, 384), ap("ES", 144, 240), ap("NN", 96, 192), AL.subtract)
+    giving(48, 144, ap("ES", 240, 336), ap("ZM", 0, 96))
+    for t in (1, 2):
+        act(ap("s80", 80 * t, 80 * t + 80), ap("ZM", 48 * t - 48, 48 * t, ind=DUP), AF.Identity, -400.0)
+    tt(ap("WZ", 400, 688), ap("ES", 96, 384), ap("MK", 0, 288), AL.mult)
+    first(2500.0)
+    scan(ap("ZO"), ap("KP", 0, 288), ap("WZ", 400, 688), 0.0, AL.mult, AL.add)
+    first(2500.0)
+    cp(ap("tz", 6, 18), ap("ZO", 7, 96, 8))
+    tt(ap("jk", 0, 96), ap("ES", 96, 192), m16(96), AL.mult)
+    scan(ap("jk", 96, 192), m16(96, "KP"), ap("jk", 0, 96), 0.0, AL.mult, AL.add)
+    cp(ap("tz", 24, 27), ap("jk", 111, 144, 16))
+    cp(ap("tz", 28, 31), ap("jk", 159, 192, 16))
+    act(ap("src", 0, 32), st(0, 32), AF.Copy)
+    act(ap("z2"), ap("src", 0, 48, ind=DUP), AF.Identity, 400.0)
+    act(ap("T1", 0, 80), ap("ES", 240, 288, ind=RZ2), AF.Identity, None, 1023.0)
+    tt(ap("T2", 0, 80), ap("T1", 0, 80), ap("z2"), AL.add)
+    tt(ap("vm", 0, 80), ap("T2", 0, 80), ap("lev"), AL.add)
+    tt(ap("vs", 0, 80), ap("T2", 0, 80), ap("g80"), AL.min)
+    lin(ap("ww"), ap("uu"), 0.04, 282.0)
+    tt(ap("tr", 0, 96), ap("ww"), ap("uu"), AL.min)
+    tt(ap("ww"), ap("tr", 0, 96), ap("ES", 240, 336), AL.max)
+    for t in (1, 2):
+        lin(ap("uu", 48 * t - 48, 48 * t), st(t + 1), 1023.0, 400.0 + 524288.0 * t)
+        v0 = ap("V0", 96 * t - 96, 96 * t - 48)
+        tt(v0, ap("uu", 48 * t - 48, 48 * t), ap("ww", 48 * t - 48, 48 * t), AL.add)
+        tt(ap("vm", 80 * t, 80 * t + 80), ap("V0", v0[1], v0[2], ind=DUP), ap("lev"), AL.add)
+        act(ap("vs", 80 * t, 80 * t + 80), ap("V0", v0[1], v0[1] + 96, ind=DUP2), AF.Copy)
+    tt(ap("g2", 0, 80), ap("ES", 96, 144, ind=RZ2), m16(80), AL.mult)
+    tt(ap("g2", 96, 176), ap("ES", 240, 288, ind=RZ2), m16(80), AL.mult)
+    scan(ap("o2", 0, 80), m16(80, "KP"), ap("g2", 0, 80), 0.0, AL.mult, AL.add)
+    scan(ap("o2", 96, 176), m16(80, "KP"), ap("g2", 96, 176), 0.0, AL.mult, AL.add)
+
+    def ow(k, t, n):
+        return ap("ow", 20 * k + 6 * t, 20 * k + 6 * t + n)
+
+    def moves(t, n, e0, s0, e1, s1):
+        tt(ow(4, t, n), e0, s0, AL.subtract)
+        ts(ow(5, t, n), ow(4, t, n), 2.0, AL.is_le, 800.0, AL.mult)
+        tt(ow(6, t, n), e1, ow(5, t, n), AL.subtract)
+        tt(ow(7, t, n), s1, s0, AL.subtract)
+        tt(ow(8, t, n), e1, s1, AL.is_equal)
+        tt(ow(9, t, n), ow(8, t, n), ow(10, 0, n), AL.mult)
+        tt(ow(3, t, n), ow(9, t, n), s1, AL.max)
+    moves(0, 5, ap("ZB", 7, 47, 8), ap("ZB", 55, 95, 8), ap("o2", 15, 80, 16), ap("o2", 111, 176, 16))
+    moves(1, 12, ap("ZO", 7, 96, 8), ap("ZO", 151, 240, 8), ap("ZO", 55, 144, 8), ap("ZO", 199, 288, 8))
+    for t in range(3):
+        ts(ap("tz", 40 + 6 * t, 45 + 6 * t), ow(3, t, 5), cf(26) if t == 1 else cf(SO), AL.add)
+
+    for t in range(3):
+        nj, nb = NJ[t], NB[t]
+        n16 = 16 * nb
+        E80, E48 = ap("tz", 6 * t, 6 * t + nb), ap("tz", 20 + 4 * t, 23 + 4 * t)
+        X, Xn, W = "XW%d" % (t % 2), "XW%d" % (1 - t % 2), "WZ"
+        qx, sx, LA = "qx%d" % t, "sx%d" % t, ap("LA%d" % t, 0, nj // 4)
+        R = [ap("R0", 0, 320), ap(W, 0, 320), ap(W, 2400, 2720)][t]
+        lo, hi = (1600, 3200) if t == 1 else (0, 2400)
+        cp(ap(W, lo, hi, ind=ap("tz", 40 + 6 * t, 45 + 6 * t)), ap("vs", 80 * t, 80 * t + 80))
+        first(3000.0 if t else 0.0)
+        quant(ap(qx), ap(sx), ap(X, 0, 1280))
+        mm(ap("pB", 0, C), ap("qp"), ap("sp"), ap(qx), ap(sx))
+        first()
+        mm(ap("pA", 0, C), ap("qp"), ap("sp"), ap(qx), ap(sx))
+        if near[t]:
+            ql, sl = "ql%d" % t, "sl%d" % t
+            send(t, ap(qx, cast=dt.uint8), ap(ql, cast=dt.uint8), 2500)
+            send(t, ap(sx), ap(sl), 2300)
+            for b in range(4):
+                e = (128 * b, 128 * b + 128)
+                mm(ap("pC%d" % b, 0, C), ap("qe", *e), ap("se", *e), ap(ql), ap(sl))
+                act(ap("DW", b, 1280, 4), ap("pC%d" % b, 0, C), AF.Copy)
+        lin(ap("SP"), ap("pA", 0, C), cf(SIG))
+        scan(ap("Mx", 1, 321), R, ap("pB", 0, C), 0.0, AL.add, AL.max)
+        first()
+        scan(ap("M", 1, 321), R, ap("SP"), 0.0, AL.add, AL.max)
+        tt(ap("Vr"), ap("M", 0, 321, ind=E48), ap("va", 48 * t, 48 * t + 48), AL.min)
+        first()
+        tt(ap("yv", 0, 8 * nb), ap("Vr", 0, 8 * nb), ap("MK", 0, 8 * nb), AL.mult)
+        first()
+        scan(ap("Vo", 0, 8 * nb), ap("KP", 0, 8 * nb), ap("yv", 0, 8 * nb), 0.0, AL.mult, AL.add)
+        first()
+        act(ap("nMx", 0, n16), ap("Mx", 0, 321, ind=E80), AF.Identity, cf(BGB), cf(NSG))
+        first()
+        for m in range(nb):
+            act(ap("tb", 41 * m, 41 * m + 40), ap("Vr", 0, 40), AF.Sign, col("Vo", 8 * m + 7), -1.0, col("sm5", 112 + m))
+        act(ap("ab", 0, 41 * nb), ap("tb", 0, 41 * nb), AF.Abs)
+        tt(ap("nr"), ap("M", 1, 321), ap("M", 0, 320), AL.is_equal)
+        scan(ap("PS", 1, 321), ap("nr"), ap("cm"), 0.0, AL.mult, AL.min)
+        tt(ap("val0", 0, n16), ap("M", 0, 321, ind=E80), ap("nMx", 0, n16), AL.is_equal)
+        tt(ap("st2", 0, n16), ap("val0", 0, n16), ap("s80", 80 * t, 80 * t + n16), AL.add)
+        tt(ap("val", 0, n16), ap("PS", 0, 321, ind=E80), ap("st2", 0, n16), AL.max)
+        scan(ap("Fs", 0, 41 * nb), ap("fl", 0, 41 * nb), ap("ab", 0, 41 * nb), 0.0, AL.mult, AL.add)
+        tt(ap("sm5", 120, 120 + nb), ap("Fs", 40, 41 * nb, 41), ap("sm5", 112, 112 + nb), AL.subtract)
+        RT = ap("tabs", 40, 40 + nb)
+        cp(RT, ap("sm5", 120, 120 + nb))
+        cp(ap("erow", ind=RT), ap("val", 0, n16))
+        tt(ap("y2", 0, nj), ap("erow", 0, nj), ap("D4", 0, nj), AL.mult)
+        scan(ap("z2", 0, nj), ap("K4", 0, nj), ap("y2", 0, nj), 0.0, AL.mult, AL.add)
+        ts(LA, ap("z2", 3, nj, 4), 4.0, AL.mult, cf(C16), AL.add)
+        A = ap("At", 0, 4 * nj)
+        if near[t]:
+            LB = ap("LB%d" % t, 0, nj // 4)
+            send(t, LA, LB, 1800)
+            act(A, ap(X, 0, 1288, ind=LA), AF.Copy)
+            lin(ap("Ah", 0, 4 * nj), A, 0.5)
+            tt(ap("Mt", 0, 4 * nj), ap("DW", ind=LB), ap("Ah", 0, 4 * nj), AL.add)
+        else:
+            hl = nj // 8 + 1
+            cp(ap("At", 0, 16 * hl), ap(X, 0, 1288, ind=ap(LA[0], 0, hl)))
+            act(ap("At", 16 * hl, 4 * nj), ap(X, 0, 1288, ind=ap(LA[0], hl, nj // 4)), AF.Copy)
+            quant(ap("qa"), ap("sa"), ap("At"))
+            send(t, ap("qa", 0, nj, cast=dt.uint8), ap("ql2", 80 - nj, 80, cast=dt.uint8), 2600)
+            send(t, ap("sa", 0, nj), ap("sl2", 80 - nj, 80), 2400)
+            lin(ap("Ah", 0, 4 * nj), A, 0.5)
+            for b in range(4):
+                e = (128 * b, 128 * b + 128)
+                mm(ap("pC%d" % b, 0, 128), ap("qe", *e), ap("se", *e), ap("ql2", 80 - nj, 208 - nj), ap("sl2", 80 - nj, 208 - nj))
+                tt(ap("Mt", b, 4 * nj, 4), ap("pC%d" % b, 0, nj), ap("Ah", b, 4 * nj, 4), AL.add)
+        quant(ap("qm"), ap("sm"), ap("Mt"))
+        for b in range(4):
+            e = (128 * b, 128 * b + 128)
+            mm(ap("pC%d" % b, 0, 128), ap("qw", *e), ap("sw", *e), ap("qm"), ap("sm"))
+            act(ap("Rr", 80 * b, 80 * b + nj), ap("pC%d" % b, 0, nj), AF.Relu, None, 0.03125)
+            for s in range(2):
+                o = 1288 + 160 * s + b
+                tt(ap(X, o, o + 2 * nj - 3, 4), ap("Rr", 80 * b + s, 80 * b + nj, 2), ap("At", 4 * s + b, 4 * nj, 8), AL.add)
+        tt(ap("val0"), ap("val", 0, 80), ap("D16"), AL.mult)
+        scan(ap("T3", 0, 80), m16(80, "KP"), ap("val0"), 0.0, AL.mult, AL.add)
+        tr(ap("T1"), ap("T3"))
+        ts(ap("T2"), ap("T1", ind=SW), -1.0, AL.mult)
+        tr(ap("T1"), ap("T2"))
+
+        def sb(k):
+            return ap("ow", 220 + 6 * k, 220 + 6 * k + nb)
+        tt(sb(3), ap("T3", 15, n16, 16), ap("T1", 15, n16, 16), AL.min)
+        ts(sb(4), sb(3), cf(SIG), AL.mult, cf(N4), AL.add)
+        tt(sb(3), sb(4), ow(7, t, nb), AL.add)
+        tt(sb(4), sb(3), ow(6, t, nb), AL.is_ge)
+        tt(sb(5), sb(4), ow(10, 0, nb), AL.mult)
+        tt(sb(4), sb(5), sb(3), AL.max)
+        QT = ap("tabs", 46, 46 + nb)
+        ts(QT, sb(4), cf(QO), AL.add)
+        cp(ap(W, 800, 2400, ind=QT), ap("vm", 80 * t, 80 * t + n16))
+        scan(ap("nr"), ap(W, 800, 1120), ap(W, 1600, 1920), 0.0, AL.max, AL.max)
+        for h in range(4):
+            if h % 2:
+                lin(ap("ym", h, 320, 4), ap("nr", h, 320, 4), cf(MH + h))
+            else:
+                ts(ap("ym", h, 320, 4), ap("nr", h, 320, 4), cf(MH + h), AL.mult)
+        scan(ap("L2"), ap("K4"), ap("ym"), 0.0, AL.mult, AL.add)
+        tt(ap("li"), ap("L2", 3, 320, 4), ap("x80"), AL.add)
+        ts(ap("lj"), ap("li"), 4095, AL.bitwise_and)
+        cp(ap("LX"), ap("lj"))
+        cp(ap(Xn, 0, 16 * XV), ap(X, ind=ap("LX", 0, XV)))
+        act(ap(Xn, 16 * XV, 1280), ap(X, ind=ap("LX", XV, 80)), AF.Copy)
+
+    quant(ap("qx3"), ap("sx3"), ap("XW1", 0, 1280))
+    mm(ap("pA", 0, C), ap("qv"), ap("sv"), ap("qx3"), ap("sx3"))
+    cp(ap("SP"), ap("pA", 0, C))
+    dma("S", "oc", [], [ap("qx3")])
+    for k in range(4):
+        dma("YS"[k % 2], "os%d" % k, [], [ap("sx3")])
+    dma("Y", "y", [], [ap("SP")])
+    dma("Y", "oz", [], [nn(3, 40)])
+    first(20000.0)
+    return ops
+
+
+def meets(a, b):
+    if a[0] != b[0] or a[1] >= b[2] or b[1] >= a[2]:
+        return False
+    if a[3] == b[3] and a[3] > 1 and a[4] is None and b[4] is None:
+        return (a[1] - b[1]) % a[3] == 0
+    return True
+
+
+def order(ops):
+    n = len(ops)
+    deps = [set() for k in range(n)]
+    seen = {}
+    for k, o in enumerate(ops):
+        if "after" in o:
+            deps[k].add(o["after"])
+        for a in o["rd"]:
+            for j, b, w in seen.get(a[0], []):
+                if w and meets(a, b):
+                    deps[k].add(j)
+        for a in o["wr"]:
+            for j, b, w in seen.get(a[0], []):
+                if meets(a, b):
+                    deps[k].add(j)
+        for a in o["rd"]:
+            seen.setdefault(a[0], []).append((k, a, False))
+        for a in o["wr"]:
+            seen.setdefault(a[0], []).append((k, a, True))
+        deps[k].discard(k)
+    hop = 60.0
+    tail = [0.0] * n
+    for k in range(n - 1, -1, -1):
+        tail[k] += ops[k]["ns"] + ops[k]["lat"] + hop
+        for j in deps[k]:
+            tail[j] = max(tail[j], tail[k])
+    tail = [tail[k] + ops[k]["up"] for k in range(n)]
+    done, free, seq = {}, {}, []
+    left = set(range(n))
+    while left:
+        best = None
+        cand = {}
+        for k in left:
+            if all(j in done for j in deps[k]):
+                cand.setdefault(ops[k]["q"], []).append((max([done[j] + hop for j in deps[k]] + [0.0]), k))
+        for q, c in cand.items():
+            now = 0.0 if q == "R" else free.get(q, 0.0)
+            now = max(now, min(r for r, k in c))
+            go = max((x for x in c if x[0] <= now), key=lambda x: (tail[x[1]], -x[1]))
+            for r, k in sorted(c):
+                if now < r < now + ops[go[1]]["ns"] and tail[k] - tail[go[1]] > ops[go[1]]["ns"] + 2 * (r - now):
+                    go = (r, k)
+                    break
+            s = max(now, go[0])
+            if best is None or s < best[0]:
+                best = (s, go[1])
+        s, k = best
+        free[ops[k]["q"]] = s + ops[k]["ns"]
+        done[k] = s + ops[k]["ns"] + ops[k]["lat"]
+        ops[k]["at"] = s
+        seq.append(k)
+        left.discard(k)
+    return seq, deps
+
+
+def waits(ops, seq, deps):
+    place, cnt = {}, {}
+    for k in seq:
+        q = ops[k]["q"]
+        cnt[q] = cnt.get(q, 0) + 1
+        place[k] = cnt[q]
+    known, clock, need = {}, {}, {}
+    for k in seq:
+        o = ops[k]
+        if o["q"] == "R":
+            clock[k] = {("one", k): 1}
+            continue
+        kn = known.setdefault(o["q"], {})
+        need[k] = []
+        for j in sorted(deps[k], key=lambda j: -ops[j]["at"]):
+            single = ops[j]["kind"] in ("dma", "recv", "send")
+            key, v = (("one", j), 1) if single else (ops[j]["q"], place[j])
+            if kn.get(key, 0) >= v:
+                continue
+            need[k].append(j)
+            for a, b in clock[j].items():
+                kn[a] = max(kn.get(a, 0), b)
+        clock[k] = dict(kn)
+        if o["kind"] in ("dma", "send"):
+            clock[k][("one", k)] = 1
+        else:
+            clock[k][o["q"]] = place[k]
+    return need
+
+
+PLANS = {}
+
+
+def rank_program(g, core, T, topo):
+    rank = T.rank_of(core)
+    if rank is None:
+        return
+    mate = [T.cores[rank ^ s] for s in STEP]
+    near = tuple(all(topo.chip(T.cores[r]) == topo.chip(T.cores[r ^ s]) for r in range(len(T.cores))) for s in STEP)
+    if near not in PLANS:
+        ops = build(near)
+        seq, deps = order(ops)
+        PLANS[near] = (ops, seq, waits(ops, seq, deps))
+    ops, seq, need = PLANS[near]
+    eng = {"V": g.vector, "S": g.scalar, "P": g.tensor, "G": g, "Y": g.sync}
+    marked = set(j for k in need for j in need[k])
+    num, cnt = {}, {}
+    for k in seq:
+        if k in marked and ops[k]["kind"] not in ("dma", "recv", "send"):
+            cnt[ops[k]["q"]] = cnt.get(ops[k]["q"], 0) + 1
+            num[k] = cnt[ops[k]["q"]]
+
+    def view(a):
+        if not isinstance(a, tuple):
+            return a
+        v = T[a[0]][:, a[1]:a[2]:a[3]] if a[3] > 1 else T[a[0]][:, a[1]:a[2]]
+        if a[5] is not None:
+            v = v.bitcast(a[5])
+        if a[4] is not None:
+            v = v.indirect(view(a[4]))
+        return v
+
+    def engines(t):
+        return len(topo.engines(core, mate[t]))
+
+    sent = 0
+    for k in seq:
+        o = ops[k]
+        if o["q"] == "R":
+            continue
+        e = eng[o["q"]]
+        for j in need[k]:
+            d = ops[j]
+            if d["kind"] == "dma":
+                e.wait_ge(T.sem["d" + d["args"]], 16)
+            elif d["kind"] == "recv":
+                e.wait_ge(T.sem["r%d" % d["args"][1]], engines(d["args"][0]))
+            else:
+                e.wait_ge(T.sem["e" + d["q"]], num[j])
+        kind, a = o["kind"], o["args"]
+        if kind == "dma":
+            if a == "x":
+                i = e.dma_start(T.XW0[:, 0:1280], T.x[:])
+            elif a == "u":
+                i = e.dma_start(T.ut[:], T.u[:])
+            elif a == "v":
+                i = e.dma_start(T.vt[:], T.v[:])
+            elif a == "z":
+                i = e.dma_start(T.zi[:], T.z[:])
+            elif a == "wc":
+                i = e.dma_start(T.qw[:].bitcast(dt.uint8), T.wc[:])
+            elif a == "ws":
+                i = e.dma_start(T.sw[:], T.ws[:])
+            elif a == "y":
+                i = e.dma_start(T.y[:], T.SP[:])
+            elif a == "oc":
+                i = e.dma_start(T.oc[:], T.qx3[:].bitcast(dt.uint8))
+            elif a == "oz":
+                i = e.dma_start(T.oz[:], T.NN[0:128:16, 144:184])
+            else:
+                m = int(a[2])
+                i = e.dma_start(T.osc[4 * m:4 * m + 4, :], T.sx3[32 * m:32 * m + 4, :])
+            i.then_inc(T.sem["d" + a], 16)
+            continue
+        if kind == "send":
+            rid, pid, se = topo.addr(mate[a[0]])
+            g.remote_dma(view(a[2]), view(a[1]), T.sem["r%d" % a[3]], T.sem.sent, pid, rid, topo.mask(core, mate[a[0]]))
+            sent += engines(a[0])
+            continue
+        v = [view(x) for x in a]
+        if kind == "activation":
+            kw = {}
+            if v[3] is not None:
+                kw["bias"] = v[3]
+            if v[4] is not None:
+                kw["scale"] = v[4]
+            if v[5] is not None:
+                kw["accum_out"] = v[5]
+            i = e.activation(v[0], v[1], v[2], **kw)
+        elif kind == "iota":
+            if SCRATCH[a[0][0]][2] == I32:
+                i = g.iota(*v)
+            else:
+                i = g.iota(*v, allow_small_or_imprecise_dtypes=True)
+        elif kind == "affine_select":
+            i = g.affine_select(*v)
+        elif kind == "matmul_mx":
+            i = e.matmul_mx(*v)
+        elif kind == "tensor_tensor":
+            i = e.tensor_tensor(*v)
+        elif kind == "tensor_scalar":
+            i = e.tensor_scalar(*v)
+        elif kind == "tensor_copy":
+            i = e.tensor_copy(*v)
+        elif kind == "tensor_tensor_scan":
+            i = e.tensor_tensor_scan(*v)
+        elif kind == "memset":
+            i = e.memset(*v)
+        elif kind == "transpose":
+            i = e.transpose(*v)
+        else:
+            i = e.quantize_mx(*v)
+        if k in num:
+            i.then_inc(T.sem["e" + o["q"]], 1)
+    g.wait_ge(T.sem.sent, sent)
+    for k in DMAS[6:]:
+        g.sync.wait_ge(T.sem["d" + k], 16)

@@ -4,9 +4,11 @@ C = 320
 NJ = [64, 72, 72]
 NB = [4, 5, 5]
 STEP = [1, 2, 4]
-XV = 40
+XS = [32, 36, 40]
 F32, BF, I32, U16, Q8, U8 = "float32", "bfloat16", "int32", "uint16", "float8_e4m3fn_x4", "uint8"
 BIG = 1e29
+HOP = 80.0
+TRIES = 900
 
 SCRATCH = {}
 
@@ -42,7 +44,7 @@ _decl("CF", 32, F32)
 _decl("zb zT", 64, F32)
 _decl("MK KP io", 384, F32)
 _decl("D16 D4 lev ctab nMx st2 val0 erow y2 z2 g80 x80", 80, F32)
-_decl("val T1 T2 T3 vb uu ww src", 96, F32)
+_decl("val T1 T2 T3 vb uu ww src V1", 96, F32)
 _decl("tb ab fl Fs io3", 208, BF)
 _decl("kk Vr yv Vo", 48, F32)
 _decl("NN va tr jk V0 g2 o2", 192, F32)
@@ -53,7 +55,7 @@ _decl("ZA ZB ZC SR sm5", 128, F32)
 _decl("ow", 256, F32)
 _decl("li lj", 80, I32)
 
-DMAS = ["x", "u", "z", "wc", "ws", "v", "y", "oc", "oz", "os0", "os1", "os2", "os3"]
+DMAS = ["pq", "ps", "x", "u", "z", "wc", "ws", "v", "y", "oc", "oz", "os0", "os1", "os2", "os3"]
 SEMAPHORES = ["eV", "eS", "eP", "eG", "sent"] + ["d" + k for k in DMAS] + ["r%d" % k for k in range(8)]
 
 
@@ -158,11 +160,11 @@ def build(near):
         rn[0] += 1
 
     dma("S", "z", [ap("zi")], [])
-    first(9000.0)
+    first(90000.0)
     dma("Y", "x", [ap("XW0", 0, 1280)], [], 2600)
-    first(9000.0)
+    first(90000.0)
     dma("S", "u", [ap("ut")], [], 2200)
-    first(9000.0)
+    first(80000.0)
     dma("Y", "wc", [ap("qw")], [], 3500)
     first(30000.0)
     dma("Y", "ws", [ap("sw")], [], 3500)
@@ -172,7 +174,7 @@ def build(near):
 
     P3, SG, H8, P16, P32, H, I8, X4, SIG, NSG, BGB, THR, C16, RZB, QO, SO, I2, N4, MH = range(19)
     iota(col("pI", 0), [[0, 1]], 0, 1)
-    first()
+    first(9000.0)
     p = col("pI", 0)
     ts(col("CI", P3), p, 3, AL.bitwise_and)
     ts(col("CI", SG), p, 2, AL.logical_shift_right, 1, AL.bitwise_and)
@@ -199,9 +201,9 @@ def build(near):
     lin(cf(N4), cf(SG), -1.0, 400.0)
     iota(ap("ctab"), [[16, 80]], 0)
     iota(ap("io", 0, 96), [[0, 12], [1, 8]], 0)
-    iota(ap("io", 96, 288), [[0, 24], [1, 8]], 0)
+    iota(ap("io", 96, 192), [[0, 12], [1, 8]], 0)
     iota(ap("io", 288, 384), [[0, 6], [1, 16]], 0)
-    for lo, hi, k in ((0, 96, I8), (96, 288, I8), (288, 384, P16)):
+    for lo, hi, k in ((0, 96, I8), (96, 192, I8), (288, 384, P16)):
         ts(ap("MK", lo, hi), ap("io", lo, hi), cf(k), AL.is_equal)
         act(ap("KP", lo, hi), ap("io", lo, hi), AF.Sign)
 
@@ -229,8 +231,7 @@ def build(near):
     lin(col("sm5", 30), cf(SG), 48.0)
     ts(DUP2, ap("sm5", 16, 21), col("sm5", 30), AL.add)
     lin(ap("tb", 40, 205, 41), ap("ctab", 0, 5), 1.0, cf(I2))
-    for k in range(2):
-        lin(ap("ow", 200 + 6 * k, 206 + 6 * k), K6, 1.0, 704.0)
+    lin(ap("ow", 200, 206), K6, 1.0, 704.0)
     lin(ap("sm5", 8, 12), ap("ow", 200, 204), cf(SG))
     lin(ap("T2", 0, 80), ap("ctab"), 1.0, cf(P16))
     lin(ap("x80"), ap("T2", 0, 80), 1.0, -1600.0)
@@ -244,29 +245,31 @@ def build(near):
     lin(ap("V0", 144, 192), ap("kk"), 0.0, -BIG)
     lin(ap("g80"), ap("lev"), -BIG, 1.5 * BIG)
     for k in range(2):
-        fill(ap("R0", 160 * k, 160 * k + 160))
-        mset(ap("XW%d" % k, 1280, 1608), 0.0)
+        fill(ap("XW%d" % k, 1280, 1444))
+        fill(ap("XW%d" % k, 1444, 1608))
+        fill(ap("Mt", 256 + 128 * k, 384 + 128 * k))
+        fill(ap("At", 256 + 128 * k, 384 + 128 * k))
     fill(ap("DW", 1280, 1288))
     for k in ("M", "Mx", "PS"):
         mset(ap(k, 0, 1), -400.0)
     fill(ap("val", 64, 96))
     fill(ap("T3", 80, 96))
-    mset(ap("Mt"), 0.0)
-    first(20000.0)
+    mset(ap("R0", 0, 320), 0.0)
+    first(9000.0)
     fill(ap("NN", 32, 48))
     fill(ap("vb", 38, 48))
     fill(ap("vb", 32, 33), 34)
     fill(ap("SR", 40, 48))
     fill(ap("SR", 104, 112))
     mset(ap("Eb"), 0.5)
+    first(20000.0)
     rec("G", "affine_select", (ap("Eb"), ap("Eb"), [[-1, 516]], AL.is_equal, 0.0, 3, 4), [ap("Eb")], [ap("Eb")], 1200)
+    first(6000.0)
     for b in range(4):
         quant(ap("qe", 128 * b, 128 * b + 128), ap("se", 128 * b, 128 * b + 128), ap("Eb", 3 - b, 515 - b))
+        first(5000.0)
     for lo in (0, 160, 800, 960, 1600, 1760, 2400, 2560):
         fill(ap("WZ", lo, lo + 160))
-    if not all(near):
-        mset(ap("At", 256, 512), 0.0)
-        quant(ap("ql2", 80, 208), ap("sl2", 80, 208), ap("Mt"))
 
     quant(ap("qu"), ap("su"), ap("ut"))
     cp(ap("qp", cast=dt.uint32), ap("qu", ind=UT, cast=dt.uint32))
@@ -283,11 +286,11 @@ def build(near):
         return ap("NN", 48 * t, 48 * t + n)
 
     def en(t, n=48):
-        o = 0 if t == 0 else 48 + 48 * t
+        o = (0, 96, 144, 288)[t]
         return ap("ES", o, o + n)
 
     def st(t, n=48):
-        o = 48 if t == 0 else 192 + 48 * t
+        o = (48, 192, 240, 336)[t]
         return ap("ES", o, o + n)
     scan(en(0), nn(0), nn(0), 0.0, AL.add, AL.max)
     tt(st(0), en(0), nn(0), AL.subtract)
@@ -335,15 +338,14 @@ def build(near):
     act(nn(3), ap("SR", 0, 48), AF.Relu, -6.0)
     for t in (1, 2, 3):
         scan(en(t), nn(t), nn(t), 0.0, AL.add, AL.max)
-    tt(st(1), en(1), nn(1), AL.subtract)
-    tt(ap("ES", 288, 384), ap("ES", 144, 240), ap("NN", 96, 192), AL.subtract)
-    giving(48, 144, ap("ES", 240, 336), ap("ZM", 0, 96))
+        tt(st(t), en(t), nn(t), AL.subtract)
     for t in (1, 2):
+        giving(48 * t, 48 * t + 48, st(t), ap("ZM", 48 * t - 48, 48 * t))
         act(ap("s80", 80 * t, 80 * t + 80), ap("ZM", 48 * t - 48, 48 * t, ind=DUP), AF.Identity, -400.0)
-    tt(ap("WZ", 400, 688), ap("ES", 96, 384), ap("MK", 0, 288), AL.mult)
-    first(2500.0)
-    scan(ap("ZO"), ap("KP", 0, 288), ap("WZ", 400, 688), 0.0, AL.mult, AL.add)
-    first(2500.0)
+    tt(ap("io", 0, 192), ap("ES", 96, 288), ap("MK", 0, 192), AL.mult)
+    scan(ap("ZO", 0, 192), ap("KP", 0, 192), ap("io", 0, 192), 0.0, AL.mult, AL.add)
+    tt(ap("io", 192, 288), ap("ES", 288, 384), ap("MK", 0, 96), AL.mult)
+    scan(ap("ZO", 192, 288), ap("KP", 0, 96), ap("io", 192, 288), 0.0, AL.mult, AL.add)
     cp(ap("tz", 6, 18), ap("ZO", 7, 96, 8))
     tt(ap("jk", 0, 96), ap("ES", 96, 192), m16(96), AL.mult)
     scan(ap("jk", 96, 192), m16(96, "KP"), ap("jk", 0, 96), 0.0, AL.mult, AL.add)
@@ -351,39 +353,44 @@ def build(near):
     cp(ap("tz", 28, 31), ap("jk", 159, 192, 16))
     act(ap("src", 0, 32), st(0, 32), AF.Copy)
     act(ap("z2"), ap("src", 0, 48, ind=DUP), AF.Identity, 400.0)
-    act(ap("T1", 0, 80), ap("ES", 240, 288, ind=RZ2), AF.Identity, None, 1023.0)
+    act(ap("T1", 0, 80), ap("ES", 192, 240, ind=RZ2), AF.Identity, None, 1023.0)
     tt(ap("T2", 0, 80), ap("T1", 0, 80), ap("z2"), AL.add)
     tt(ap("vm", 0, 80), ap("T2", 0, 80), ap("lev"), AL.add)
     tt(ap("vs", 0, 80), ap("T2", 0, 80), ap("g80"), AL.min)
     lin(ap("ww"), ap("uu"), 0.04, 282.0)
     tt(ap("tr", 0, 96), ap("ww"), ap("uu"), AL.min)
-    tt(ap("ww"), ap("tr", 0, 96), ap("ES", 240, 336), AL.max)
+    tt(ap("ww"), ap("tr", 0, 96), ap("ES", 192, 288), AL.max)
     for t in (1, 2):
         lin(ap("uu", 48 * t - 48, 48 * t), st(t + 1), 1023.0, 400.0 + 524288.0 * t)
         v0 = ap("V0", 96 * t - 96, 96 * t - 48)
         tt(v0, ap("uu", 48 * t - 48, 48 * t), ap("ww", 48 * t - 48, 48 * t), AL.add)
-        tt(ap("vm", 80 * t, 80 * t + 80), ap("V0", v0[1], v0[2], ind=DUP), ap("lev"), AL.add)
+        for k in range(2):
+            lin(ap("V1", 48 * k, 48 * k + 48), v0, 1.0, 1.0 + k)
+        act(ap("vm", 80 * t, 80 * t + 80), ap("V1", ind=DUP2), AF.Copy)
         act(ap("vs", 80 * t, 80 * t + 80), ap("V0", v0[1], v0[1] + 96, ind=DUP2), AF.Copy)
     tt(ap("g2", 0, 80), ap("ES", 96, 144, ind=RZ2), m16(80), AL.mult)
-    tt(ap("g2", 96, 176), ap("ES", 240, 288, ind=RZ2), m16(80), AL.mult)
+    tt(ap("g2", 96, 176), ap("ES", 192, 240, ind=RZ2), m16(80), AL.mult)
     scan(ap("o2", 0, 80), m16(80, "KP"), ap("g2", 0, 80), 0.0, AL.mult, AL.add)
     scan(ap("o2", 96, 176), m16(80, "KP"), ap("g2", 96, 176), 0.0, AL.mult, AL.add)
 
-    def ow(k, t, n):
+    def ow(k, t, n=5):
         return ap("ow", 20 * k + 6 * t, 20 * k + 6 * t + n)
 
-    def moves(t, n, e0, s0, e1, s1):
-        tt(ow(4, t, n), e0, s0, AL.subtract)
-        ts(ow(5, t, n), ow(4, t, n), 2.0, AL.is_le, 800.0, AL.mult)
-        tt(ow(6, t, n), e1, ow(5, t, n), AL.subtract)
-        tt(ow(7, t, n), s1, s0, AL.subtract)
-        tt(ow(8, t, n), e1, s1, AL.is_equal)
-        tt(ow(9, t, n), ow(8, t, n), ow(10, 0, n), AL.mult)
-        tt(ow(3, t, n), ow(9, t, n), s1, AL.max)
-    moves(0, 5, ap("ZB", 7, 47, 8), ap("ZB", 55, 95, 8), ap("o2", 15, 80, 16), ap("o2", 111, 176, 16))
-    moves(1, 12, ap("ZO", 7, 96, 8), ap("ZO", 151, 240, 8), ap("ZO", 55, 144, 8), ap("ZO", 199, 288, 8))
-    for t in range(3):
-        ts(ap("tz", 40 + 6 * t, 45 + 6 * t), ow(3, t, 5), cf(26) if t == 1 else cf(SO), AL.add)
+    def moves(t, e0, s0, e1, s1):
+        tt(ow(4, t), e0, s0, AL.subtract)
+        ts(ow(5, t), ow(4, t), 2.0, AL.is_le, 800.0, AL.mult)
+        tt(ow(6, t), e1, ow(5, t), AL.subtract)
+        tt(ow(7, t), s1, s0, AL.subtract)
+        tt(ow(8, t), e1, s1, AL.is_equal)
+        tt(ow(9, t), ow(8, t), ow(10, 0), AL.mult)
+        tt(ow(3, t), ow(9, t), s1, AL.max)
+        ts(ap("tz", 40 + 6 * t, 45 + 6 * t), ow(3, t), cf(26) if t == 1 else cf(SO), AL.add)
+
+    def zo(o):
+        return ap("ZO", o + 7, o + 47, 8)
+    moves(0, ap("ZB", 7, 47, 8), ap("ZB", 55, 95, 8), ap("o2", 15, 80, 16), ap("o2", 111, 176, 16))
+    moves(1, zo(0), zo(96), zo(48), zo(144))
+    moves(2, zo(48), zo(144), zo(192), zo(240))
 
     for t in range(3):
         nj, nb = NJ[t], NB[t]
@@ -399,6 +406,9 @@ def build(near):
         mm(ap("pB", 0, C), ap("qp"), ap("sp"), ap(qx), ap(sx))
         first()
         mm(ap("pA", 0, C), ap("qp"), ap("sp"), ap(qx), ap(sx))
+        if t == 0:
+            dma("Y", "pq", [ap("ql2", 80, 208)], [ap(qx)])
+            dma("Y", "ps", [ap("sl2", 80, 208)], [ap(sx)])
         if near[t]:
             ql, sl = "ql%d" % t, "sl%d" % t
             send(t, ap(qx, cast=dt.uint8), ap(ql, cast=dt.uint8), 2500)
@@ -447,8 +457,8 @@ def build(near):
             cp(ap("At", 0, 16 * hl), ap(X, 0, 1288, ind=ap(LA[0], 0, hl)))
             act(ap("At", 16 * hl, 4 * nj), ap(X, 0, 1288, ind=ap(LA[0], hl, nj // 4)), AF.Copy)
             quant(ap("qa"), ap("sa"), ap("At"))
-            send(t, ap("qa", 0, nj, cast=dt.uint8), ap("ql2", 80 - nj, 80, cast=dt.uint8), 2600)
-            send(t, ap("sa", 0, nj), ap("sl2", 80 - nj, 80), 2400)
+            send(t, ap("qa", 0, nj, cast=dt.uint8), ap("ql2", 80 - nj, 80, cast=dt.uint8), 3000)
+            send(t, ap("sa", 0, nj), ap("sl2", 80 - nj, 80), 2800)
             lin(ap("Ah", 0, 4 * nj), A, 0.5)
             for b in range(4):
                 e = (128 * b, 128 * b + 128)
@@ -465,7 +475,10 @@ def build(near):
         tt(ap("val0"), ap("val", 0, 80), ap("D16"), AL.mult)
         scan(ap("T3", 0, 80), m16(80, "KP"), ap("val0"), 0.0, AL.mult, AL.add)
         tr(ap("T1"), ap("T3"))
-        ts(ap("T2"), ap("T1", ind=SW), -1.0, AL.mult)
+        if t < 2:
+            lin(ap("T2"), ap("T1", ind=SW), -1.0)
+        else:
+            ts(ap("T2"), ap("T1", ind=SW), -1.0, AL.mult)
         tr(ap("T1"), ap("T2"))
 
         def sb(k):
@@ -481,7 +494,7 @@ def build(near):
         cp(ap(W, 800, 2400, ind=QT), ap("vm", 80 * t, 80 * t + n16))
         scan(ap("nr"), ap(W, 800, 1120), ap(W, 1600, 1920), 0.0, AL.max, AL.max)
         for h in range(4):
-            if h % 2:
+            if h % 2 or t < 2:
                 lin(ap("ym", h, 320, 4), ap("nr", h, 320, 4), cf(MH + h))
             else:
                 ts(ap("ym", h, 320, 4), ap("nr", h, 320, 4), cf(MH + h), AL.mult)
@@ -489,12 +502,16 @@ def build(near):
         tt(ap("li"), ap("L2", 3, 320, 4), ap("x80"), AL.add)
         ts(ap("lj"), ap("li"), 4095, AL.bitwise_and)
         cp(ap("LX"), ap("lj"))
-        cp(ap(Xn, 0, 16 * XV), ap(X, ind=ap("LX", 0, XV)))
-        act(ap(Xn, 16 * XV, 1280), ap(X, ind=ap("LX", XV, 80)), AF.Copy)
+        xv = XS[t]
+        cp(ap(Xn, 0, 16 * xv), ap(X, ind=ap("LX", 0, xv)))
+        act(ap(Xn, 16 * xv, 1280), ap(X, ind=ap("LX", xv, 80)), AF.Copy)
 
-    quant(ap("qx3"), ap("sx3"), ap("XW1", 0, 1280))
-    mm(ap("pA", 0, C), ap("qv"), ap("sv"), ap("qx3"), ap("sx3"))
-    cp(ap("SP"), ap("pA", 0, C))
+    for k in range(2):
+        c = (160 * k, 160 * k + 160)
+        quant(ap("qx3", *c), ap("sx3", *c), ap("XW1", 4 * c[0], 4 * c[1]))
+        mm(ap("pA" if k else "pB", 0, 160), ap("qv"), ap("sv"), ap("qx3", *c), ap("sx3", *c))
+    act(ap("SP", 0, 160), ap("pB", 0, 160), AF.Copy)
+    cp(ap("SP", 160, 320), ap("pA", 0, 160))
     dma("S", "oc", [], [ap("qx3")])
     for k in range(4):
         dma("YS"[k % 2], "os%d" % k, [], [ap("sx3")])
@@ -512,7 +529,7 @@ def meets(a, b):
     return True
 
 
-def order(ops):
+def depends(ops):
     n = len(ops)
     deps = [set() for k in range(n)]
     seen = {}
@@ -532,39 +549,75 @@ def order(ops):
         for a in o["wr"]:
             seen.setdefault(a[0], []).append((k, a, True))
         deps[k].discard(k)
-    hop = 60.0
     tail = [0.0] * n
     for k in range(n - 1, -1, -1):
-        tail[k] += ops[k]["ns"] + ops[k]["lat"] + hop
+        tail[k] += ops[k]["ns"] + ops[k]["lat"] + HOP
         for j in deps[k]:
             tail[j] = max(tail[j], tail[k])
-    tail = [tail[k] + ops[k]["up"] for k in range(n)]
-    done, free, seq = {}, {}, []
-    left = set(range(n))
-    while left:
+    return deps, [tail[k] + ops[k]["up"] for k in range(n)]
+
+
+def arrange(ops, deps, tail):
+    n = len(ops)
+    users = [[] for k in range(n)]
+    for k in range(n):
+        for j in deps[k]:
+            users[j].append(k)
+    miss = [len(d) for d in deps]
+    ready = [0.0] * n
+    cand, free, seq, at, end = {}, {}, [], [0.0] * n, 0.0
+    for k in range(n):
+        if not miss[k]:
+            cand.setdefault(ops[k]["q"], []).append(k)
+    while len(seq) < n:
         best = None
-        cand = {}
-        for k in left:
-            if all(j in done for j in deps[k]):
-                cand.setdefault(ops[k]["q"], []).append((max([done[j] + hop for j in deps[k]] + [0.0]), k))
         for q, c in cand.items():
+            if not c:
+                continue
             now = 0.0 if q == "R" else free.get(q, 0.0)
-            now = max(now, min(r for r, k in c))
-            go = max((x for x in c if x[0] <= now), key=lambda x: (tail[x[1]], -x[1]))
-            for r, k in sorted(c):
-                if now < r < now + ops[go[1]]["ns"] and tail[k] - tail[go[1]] > ops[go[1]]["ns"] + 2 * (r - now):
-                    go = (r, k)
-                    break
-            s = max(now, go[0])
+            now = max(now, min(ready[k] for k in c))
+            go = max((k for k in c if ready[k] <= now), key=lambda k: (tail[k], -k))
+            ns = ops[go]["ns"]
+            late = [k for k in c if now < ready[k] < now + ns and tail[k] - tail[go] > ns + 2 * (ready[k] - now)]
+            if late:
+                go = min(late, key=lambda k: (ready[k], k))
+            s = max(now, ready[go])
             if best is None or s < best[0]:
-                best = (s, go[1])
+                best = (s, go)
         s, k = best
-        free[ops[k]["q"]] = s + ops[k]["ns"]
-        done[k] = s + ops[k]["ns"] + ops[k]["lat"]
-        ops[k]["at"] = s
+        o = ops[k]
+        cand[o["q"]].remove(k)
+        free[o["q"]] = s + o["ns"]
+        done = s + o["ns"] + o["lat"]
+        end = max(end, done)
+        at[k] = s
         seq.append(k)
-        left.discard(k)
-    return seq, deps
+        for j in users[k]:
+            ready[j] = max(ready[j], done + HOP)
+            miss[j] -= 1
+            if not miss[j]:
+                cand.setdefault(ops[j]["q"], []).append(j)
+    return end, seq, at
+
+
+def order(ops):
+    deps, tail = depends(ops)
+    best = arrange(ops, deps, tail)
+    r = [12345]
+
+    def draw(m):
+        r[0] = (r[0] * 1103515245 + 12345) % 2147483648
+        return (r[0] >> 8) % m
+    for i in range(TRIES):
+        other = list(tail)
+        for j in range(1 << draw(4)):
+            other[draw(len(ops))] += (200.0, 600.0, 1500.0, 4000.0)[draw(4)] * (1 - 2 * draw(2))
+        got = arrange(ops, deps, other)
+        if got[0] <= best[0]:
+            best, tail = got, other
+    for k, o in enumerate(ops):
+        o["at"] = best[2][k]
+    return best[1], deps
 
 
 def waits(ops, seq, deps):
@@ -632,6 +685,17 @@ def rank_program(g, core, T, topo):
     def engines(t):
         return len(topo.engines(core, mate[t]))
 
+    u8 = dt.uint8
+    sides = {"pq": (T.ql2[:, 80:208].bitcast(u8), T.qx0[:, 0:128].bitcast(u8)), "ps": (T.sl2[:, 80:208], T.sx0[:, 0:128]),
+             "x": (T.XW0[:, 0:1280], T.x[:]), "u": (T.ut[:], T.u[:]), "v": (T.vt[:], T.v[:]), "z": (T.zi[:], T.z[:]),
+             "wc": (T.qw[:].bitcast(u8), T.wc[:]), "ws": (T.sw[:], T.ws[:]), "y": (T.y[:], T.SP[:]),
+             "oc": (T.oc[:], T.qx3[:].bitcast(u8)), "oz": (T.oz[:], T.NN[0:128:16, 144:184])}
+    for m in range(4):
+        sides["os%d" % m] = (T.osc[4 * m:4 * m + 4, :], T.sx3[32 * m:32 * m + 4, :])
+    calls = {"affine_select": g.affine_select, "matmul_mx": g.tensor.matmul_mx, "tensor_tensor": g.vector.tensor_tensor,
+             "tensor_scalar": g.vector.tensor_scalar, "tensor_copy": g.vector.tensor_copy,
+             "tensor_tensor_scan": g.vector.tensor_tensor_scan, "memset": g.vector.memset,
+             "transpose": g.vector.transpose, "quantize_mx": g.vector.quantize_mx}
     sent = 0
     for k in seq:
         o = ops[k]
@@ -648,28 +712,7 @@ def rank_program(g, core, T, topo):
                 e.wait_ge(T.sem["e" + d["q"]], num[j])
         kind, a = o["kind"], o["args"]
         if kind == "dma":
-            if a == "x":
-                i = e.dma_start(T.XW0[:, 0:1280], T.x[:])
-            elif a == "u":
-                i = e.dma_start(T.ut[:], T.u[:])
-            elif a == "v":
-                i = e.dma_start(T.vt[:], T.v[:])
-            elif a == "z":
-                i = e.dma_start(T.zi[:], T.z[:])
-            elif a == "wc":
-                i = e.dma_start(T.qw[:].bitcast(dt.uint8), T.wc[:])
-            elif a == "ws":
-                i = e.dma_start(T.sw[:], T.ws[:])
-            elif a == "y":
-                i = e.dma_start(T.y[:], T.SP[:])
-            elif a == "oc":
-                i = e.dma_start(T.oc[:], T.qx3[:].bitcast(dt.uint8))
-            elif a == "oz":
-                i = e.dma_start(T.oz[:], T.NN[0:128:16, 144:184])
-            else:
-                m = int(a[2])
-                i = e.dma_start(T.osc[4 * m:4 * m + 4, :], T.sx3[32 * m:32 * m + 4, :])
-            i.then_inc(T.sem["d" + a], 16)
+            e.dma_start(*sides[a]).then_inc(T.sem["d" + a], 16)
             continue
         if kind == "send":
             rid, pid, se = topo.addr(mate[a[0]])
@@ -679,38 +722,19 @@ def rank_program(g, core, T, topo):
         v = [view(x) for x in a]
         if kind == "activation":
             kw = {}
-            if v[3] is not None:
-                kw["bias"] = v[3]
-            if v[4] is not None:
-                kw["scale"] = v[4]
-            if v[5] is not None:
-                kw["accum_out"] = v[5]
+            for name, x in zip(("bias", "scale", "accum_out"), v[3:]):
+                if x is not None:
+                    kw[name] = x
             i = e.activation(v[0], v[1], v[2], **kw)
         elif kind == "iota":
             if SCRATCH[a[0][0]][2] == I32:
                 i = g.iota(*v)
             else:
                 i = g.iota(*v, allow_small_or_imprecise_dtypes=True)
-        elif kind == "affine_select":
-            i = g.affine_select(*v)
-        elif kind == "matmul_mx":
-            i = e.matmul_mx(*v)
-        elif kind == "tensor_tensor":
-            i = e.tensor_tensor(*v)
-        elif kind == "tensor_scalar":
-            i = e.tensor_scalar(*v)
-        elif kind == "tensor_copy":
-            i = e.tensor_copy(*v)
-        elif kind == "tensor_tensor_scan":
-            i = e.tensor_tensor_scan(*v)
-        elif kind == "memset":
-            i = e.memset(*v)
-        elif kind == "transpose":
-            i = e.transpose(*v)
         else:
-            i = e.quantize_mx(*v)
+            i = calls[kind](*v)
         if k in num:
             i.then_inc(T.sem["e" + o["q"]], 1)
     g.wait_ge(T.sem.sent, sent)
-    for k in DMAS[6:]:
+    for k in DMAS[8:]:
         g.sync.wait_ge(T.sem["d" + k], 16)

@@ -7,8 +7,8 @@ STEP = [1, 2, 4]
 XS = [32, 36, 40]
 F32, BF, I32, U16, Q8, U8 = "float32", "bfloat16", "int32", "uint16", "float8_e4m3fn_x4", "uint8"
 BIG = 1e29
-HOP = 80.0
-TRIES = 900
+HOP = 90.0
+TRIES = 3500
 
 SCRATCH = {}
 
@@ -31,7 +31,7 @@ _decl("qw qe", 512, Q8)
 _decl("sw se", 512, U8)
 _decl("qu qp qv qa qm", 128, Q8)
 _decl("su sp sv sa sm", 128, U8)
-_decl("pA pB pC0 pC1 pC2 pC3", 512, F32, "psum")
+_decl("pA pB pD pE pC0 pC1 pC2 pC3", 512, F32, "psum")
 _decl("SP nr cm K4 io4 ym L2 Rr", 320, F32)
 _decl("M Mx PS", 336, F32)
 _decl("WZ", 3200, F32)
@@ -43,7 +43,7 @@ _decl("CI", 8, I32)
 _decl("CF", 32, F32)
 _decl("zb zT", 64, F32)
 _decl("MK KP io", 384, F32)
-_decl("D16 D4 lev ctab nMx st2 val0 erow y2 z2 g80 x80", 80, F32)
+_decl("D16 D4 D4b lev ctab nMx st2 val0 erow y2 z2 g80 x80", 80, F32)
 _decl("val T1 T2 T3 vb uu ww src V1", 96, F32)
 _decl("tb ab fl Fs io3", 208, BF)
 _decl("kk Vr yv Vo", 48, F32)
@@ -55,7 +55,7 @@ _decl("ZA ZB ZC SR sm5", 128, F32)
 _decl("ow", 256, F32)
 _decl("li lj", 80, I32)
 
-DMAS = ["pq", "ps", "x", "u", "z", "wc", "ws", "v", "y", "oc", "oz", "os0", "os1", "os2", "os3"]
+DMAS = ["pq", "ps", "x0", "x1", "u", "z", "wc", "ws", "v", "y0", "y1", "oc0", "oc1", "oz", "os0", "os1", "os2", "os3"]
 SEMAPHORES = ["eV", "eS", "eP", "eG", "sent"] + ["d" + k for k in DMAS] + ["r%d" % k for k in range(8)]
 
 
@@ -121,7 +121,7 @@ def build(near):
         rec("V", "tensor_copy", (out, a), [out], [a], vns(out, a, half(out, a)))
 
     def scan(out, a, b, init, op0, op1):
-        rec("V", "tensor_tensor_scan", (out, a, b, init, op0, op1), [out], [a, b], vns(out, a, half(out, a, b)))
+        rec("V", "tensor_tensor_scan", (out, a, b, init, op0, op1), [out], [a, b, init], vns(out, a, half(out, a, b)))
 
     def mset(out, v):
         rec("V", "memset", (out, v), [out], [], vns(out, out, half(out)))
@@ -133,14 +133,14 @@ def build(near):
         rec("V", "quantize_mx", (q, s, a), [q, s], [a], 20 + 0.27 * count(a))
 
     def act(out, a, f, bias=None, scale=None, acc=None):
-        n = 80 + (1.6 if a[4] is not None else 1.0) * count(a) + (25 if acc else 0)
+        n = 95 + (1.6 if a[4] is not None else 1.0) * count(a) + (25 if acc else 0)
         rec("S", "activation", (out, a, f, bias, scale, acc), [out] + ([acc] if acc else []), [a, bias, scale], n)
 
     def lin(out, a, scale, bias=None):
         act(out, a, AF.Identity, bias, scale)
 
     def mm(out, w, ws, x, xs):
-        rec("P", "matmul_mx", (out, w, ws, x, xs, True, True), [ap(out[0])], [w, ws, x, xs], 20 + 0.7 * count(x))
+        rec("P", "matmul_mx", (out, w, ws, x, xs, True, True), [ap(out[0])], [w, ws, x, xs], 20 + 0.8 * count(x))
 
     def iota(out, pat, base, ch=0):
         rec("G", "iota", (out, pat, base, ch), [out], [], 130 + 2.0 * count(out))
@@ -149,7 +149,7 @@ def build(near):
         iota(out, [[0, count(out)]], v)
 
     def dma(q, name, outs, ins, lat=2000):
-        rec(q, "dma", name, outs, ins, 60, lat)
+        rec(q, "dma", name, outs, ins, 80, lat)
 
     rn = [0]
 
@@ -161,15 +161,17 @@ def build(near):
 
     dma("S", "z", [ap("zi")], [])
     first(90000.0)
-    dma("Y", "x", [ap("XW0", 0, 1280)], [], 2600)
+    dma("Y", "x0", [ap("XW0", 0, 640)], [], 2300)
+    first(95000.0)
+    dma("Y", "x1", [ap("XW0", 640, 1280)], [], 2700)
     first(90000.0)
-    dma("S", "u", [ap("ut")], [], 2200)
+    dma("S", "u", [ap("ut")], [], 2300)
     first(80000.0)
-    dma("Y", "wc", [ap("qw")], [], 3500)
+    dma("Y", "wc", [ap("qw")], [ap("XW0", 1272, 1280)], 3500)
     first(30000.0)
-    dma("Y", "ws", [ap("sw")], [], 3500)
+    dma("Y", "ws", [ap("sw")], [ap("XW0", 1272, 1280)], 3500)
     first(30000.0)
-    dma("Y", "v", [ap("vt")], [], 3500)
+    dma("Y", "v", [ap("vt")], [ap("qw")], 3500)
     first(40000.0)
 
     P3, SG, H8, P16, P32, H, I8, X4, SIG, NSG, BGB, THR, C16, RZB, QO, SO, I2, N4, MH = range(19)
@@ -213,8 +215,8 @@ def build(near):
     for k in range(2):
         iota(ap("io4", 160 * k, 160 * k + 160), [[0, 40], [1, 4]], 0)
         iota(ap("cm", 160 * k, 160 * k + 160), [[1, 160]], 160 * k - 400)
-    ts(ap("D4"), ap("io4", 0, 80), cf(H), AL.is_equal)
-    lin(ap("CF", MH, MH + 4), ap("D4", 0, 4), 4.0)
+    ts(ap("D4b"), ap("io4", 0, 80), cf(H), AL.is_equal)
+    lin(ap("CF", MH, MH + 4), ap("D4b", 0, 4), 4.0)
     act(ap("K4"), ap("io4"), AF.Sign)
     iota(ap("io3", 0, 205), [[-8, 5], [1, 41]], 0)
     ts(ap("Fs", 0, 205), ap("io3", 0, 205), cf(I8), AL.not_equal, 2.0, AL.mult)
@@ -236,14 +238,14 @@ def build(near):
     lin(ap("T2", 0, 80), ap("ctab"), 1.0, cf(P16))
     lin(ap("x80"), ap("T2", 0, 80), 1.0, -1600.0)
     lin(ap("kk"), ap("ctab", 0, 48), 1.0 / 1024)
-    iota(ap("lev"), [[0, 10], [1, 2], [0, 4]], 1)
+    iota(ap("lev"), [[0, 10], [1, 2], [0, 4]], 0)
     iota(ap("sm5", 32, 38), [[4, 3], [0, 2]], 17)
     iota(ap("sm5", 40, 45), [[1, 5]], 0)
     act(ap("vb", 48, 96), ap("kk"), AF.Relu, -31.0, 64.0)
     act(ap("src", 32, 48), ap("kk", 32, 48), AF.Identity, 322.0 - 40 * 32, 40 * 64.0)
     lin(ap("V0", 48, 96), ap("kk"), 0.0, -BIG)
     lin(ap("V0", 144, 192), ap("kk"), 0.0, -BIG)
-    lin(ap("g80"), ap("lev"), -BIG, 1.5 * BIG)
+    lin(ap("g80"), ap("lev"), -BIG, -1.0)
     for k in range(2):
         fill(ap("XW%d" % k, 1280, 1444))
         fill(ap("XW%d" % k, 1444, 1608))
@@ -252,8 +254,7 @@ def build(near):
     fill(ap("DW", 1280, 1288))
     for k in ("M", "Mx", "PS"):
         mset(ap(k, 0, 1), -400.0)
-    fill(ap("val", 64, 96))
-    fill(ap("T3", 80, 96))
+    fill(ap("T3", 64, 96))
     mset(ap("R0", 0, 320), 0.0)
     first(9000.0)
     fill(ap("NN", 32, 48))
@@ -305,12 +306,12 @@ def build(near):
     scan(ap("o2", 0, 48), m16(48, "KP"), ap("g2", 0, 48), 0.0, AL.mult, AL.add)
     cp(ap("tz", 20, 23), ap("o2", 15, 48, 16))
 
-    def giving(lo, hi, starts, out):
+    def giving(t):
+        lo, hi = 48 * t, 48 * t + 48
         lin(ap("va", lo, hi), ap("NN", lo, hi), 1e26, cf(THR))
         ts(ap("tr", lo, hi), ap("va", lo, hi), -1.0, AL.mult, 320.0, AL.min)
-        tt(out, ap("tr", lo, hi), starts, AL.max)
-    giving(0, 48, st(0), ap("jk", 64, 112))
-    act(ap("s80", 0, 80), ap("jk", 64, 112, ind=DUP), AF.Identity, -400.0)
+        tt(ap("s80", lo, hi), ap("tr", lo, hi), st(t), AL.max)
+    giving(0)
 
     act(ap("vb", 0, 32), nn(0, 32), AF.Copy)
     for j in range(5):
@@ -327,8 +328,8 @@ def build(near):
         act(ap("ZO", 40 * m, 40 * m + 40), ap("ZC", 64, 104), AF.Sign, col("ZA", 47 + 8 * m), -1.0, col("sm5", 104 + m))
     ts(RZ, ap("sm5", 104, 109), -0.5, AL.mult, cf(RZB), AL.add)
     ts(RZ2, ap("sm5", 104, 109), -0.5, AL.mult, 19.5, AL.add)
-    act(ap("y2"), ap("vb", ind=DUP2), AF.Copy)
-    cp(ap("SR", ind=RZ), ap("y2"))
+    act(ap("D4"), ap("vb", ind=DUP2), AF.Copy)
+    cp(ap("SR", ind=RZ), ap("D4"))
     for t in (1, 2):
         u = ap("uu", 48 * t - 48, 48 * t)
         w = ap("ww", 48 * t - 48, 48 * t)
@@ -339,9 +340,8 @@ def build(near):
     for t in (1, 2, 3):
         scan(en(t), nn(t), nn(t), 0.0, AL.add, AL.max)
         tt(st(t), en(t), nn(t), AL.subtract)
-    for t in (1, 2):
-        giving(48 * t, 48 * t + 48, st(t), ap("ZM", 48 * t - 48, 48 * t))
-        act(ap("s80", 80 * t, 80 * t + 80), ap("ZM", 48 * t - 48, 48 * t, ind=DUP), AF.Identity, -400.0)
+    giving(1)
+    giving(2)
     tt(ap("io", 0, 192), ap("ES", 96, 288), ap("MK", 0, 192), AL.mult)
     scan(ap("ZO", 0, 192), ap("KP", 0, 192), ap("io", 0, 192), 0.0, AL.mult, AL.add)
     tt(ap("io", 192, 288), ap("ES", 288, 384), ap("MK", 0, 96), AL.mult)
@@ -352,14 +352,14 @@ def build(near):
     cp(ap("tz", 24, 27), ap("jk", 111, 144, 16))
     cp(ap("tz", 28, 31), ap("jk", 159, 192, 16))
     act(ap("src", 0, 32), st(0, 32), AF.Copy)
-    act(ap("z2"), ap("src", 0, 48, ind=DUP), AF.Identity, 400.0)
+    lin(ap("src", 48, 96), ap("src", 0, 48), 1.0, 1.0)
+    act(ap("z2"), ap("src", ind=DUP2), AF.Identity, 401.0)
     act(ap("T1", 0, 80), ap("ES", 192, 240, ind=RZ2), AF.Identity, None, 1023.0)
-    tt(ap("T2", 0, 80), ap("T1", 0, 80), ap("z2"), AL.add)
-    tt(ap("vm", 0, 80), ap("T2", 0, 80), ap("lev"), AL.add)
-    tt(ap("vs", 0, 80), ap("T2", 0, 80), ap("g80"), AL.min)
+    tt(ap("vm", 0, 80), ap("T1", 0, 80), ap("z2"), AL.add)
+    tt(ap("vs", 0, 80), ap("vm", 0, 80), ap("g80"), AL.add)
     lin(ap("ww"), ap("uu"), 0.04, 282.0)
-    tt(ap("tr", 0, 96), ap("ww"), ap("uu"), AL.min)
-    tt(ap("ww"), ap("tr", 0, 96), ap("ES", 192, 288), AL.max)
+    tt(ap("ZM", 0, 96), ap("ww"), ap("uu"), AL.min)
+    tt(ap("ww"), ap("ZM", 0, 96), ap("ES", 192, 288), AL.max)
     for t in (1, 2):
         lin(ap("uu", 48 * t - 48, 48 * t), st(t + 1), 1023.0, 400.0 + 524288.0 * t)
         v0 = ap("V0", 96 * t - 96, 96 * t - 48)
@@ -402,53 +402,55 @@ def build(near):
         lo, hi = (1600, 3200) if t == 1 else (0, 2400)
         cp(ap(W, lo, hi, ind=ap("tz", 40 + 6 * t, 45 + 6 * t)), ap("vs", 80 * t, 80 * t + 80))
         first(3000.0 if t else 0.0)
-        quant(ap(qx), ap(sx), ap(X, 0, 1280))
-        mm(ap("pB", 0, C), ap("qp"), ap("sp"), ap(qx), ap(sx))
-        first()
-        mm(ap("pA", 0, C), ap("qp"), ap("sp"), ap(qx), ap(sx))
-        if t == 0:
-            dma("Y", "pq", [ap("ql2", 80, 208)], [ap(qx)])
-            dma("Y", "ps", [ap("sl2", 80, 208)], [ap(sx)])
-        if near[t]:
-            ql, sl = "ql%d" % t, "sl%d" % t
-            send(t, ap(qx, cast=dt.uint8), ap(ql, cast=dt.uint8), 2500)
-            send(t, ap(sx), ap(sl), 2300)
-            for b in range(4):
-                e = (128 * b, 128 * b + 128)
-                mm(ap("pC%d" % b, 0, C), ap("qe", *e), ap("se", *e), ap(ql), ap(sl))
-                act(ap("DW", b, 1280, 4), ap("pC%d" % b, 0, C), AF.Copy)
-        lin(ap("SP"), ap("pA", 0, C), cf(SIG))
-        scan(ap("Mx", 1, 321), R, ap("pB", 0, C), 0.0, AL.add, AL.max)
-        first()
-        scan(ap("M", 1, 321), R, ap("SP"), 0.0, AL.add, AL.max)
+        for c0, c1, b0, b1 in ((0, 160, "pA", "pB"), (160, C, "pD", "pE")):
+            quant(ap(qx, c0, c1), ap(sx, c0, c1), ap(X, 4 * c0, 4 * c1))
+            for b in (b0, b1):
+                mm(ap(b, 0, c1 - c0), ap("qp"), ap("sp"), ap(qx, c0, c1), ap(sx, c0, c1))
+            lin(ap("SP", c0, c1), ap(b0, 0, c1 - c0), cf(SIG))
+            r = ap(R[0], R[1] + c0, R[1] + c1)
+            scan(ap("Mx", 1 + c0, 1 + c1), r, ap(b1, 0, c1 - c0), col("Mx", c0), AL.add, AL.max)
+            scan(ap("M", 1 + c0, 1 + c1), r, ap("SP", c0, c1), col("M", c0), AL.add, AL.max)
+            tt(ap("nr", c0, c1), ap("M", 1 + c0, 1 + c1), ap("M", c0, c1), AL.is_equal)
+        scan(ap("PS", 1, 321), ap("nr"), ap("cm"), 0.0, AL.mult, AL.min)
+        if t == 1:
+            dma("Y", "pq", [ap("ql2", 80, 208)], [ap("qx0"), ap("PS")])
+            dma("Y", "ps", [ap("sl2", 80, 208)], [ap("sx0"), ap("PS")])
         tt(ap("Vr"), ap("M", 0, 321, ind=E48), ap("va", 48 * t, 48 * t + 48), AL.min)
         first()
         tt(ap("yv", 0, 8 * nb), ap("Vr", 0, 8 * nb), ap("MK", 0, 8 * nb), AL.mult)
         first()
         scan(ap("Vo", 0, 8 * nb), ap("KP", 0, 8 * nb), ap("yv", 0, 8 * nb), 0.0, AL.mult, AL.add)
         first()
-        act(ap("nMx", 0, n16), ap("Mx", 0, 321, ind=E80), AF.Identity, cf(BGB), cf(NSG))
+        act(ap("nMx", 0, 48), ap("Mx", 0, 321, ind=E48), AF.Identity, cf(BGB), cf(NSG))
         first()
         for m in range(nb):
             act(ap("tb", 41 * m, 41 * m + 40), ap("Vr", 0, 40), AF.Sign, col("Vo", 8 * m + 7), -1.0, col("sm5", 112 + m))
         act(ap("ab", 0, 41 * nb), ap("tb", 0, 41 * nb), AF.Abs)
-        tt(ap("nr"), ap("M", 1, 321), ap("M", 0, 320), AL.is_equal)
-        scan(ap("PS", 1, 321), ap("nr"), ap("cm"), 0.0, AL.mult, AL.min)
-        tt(ap("val0", 0, n16), ap("M", 0, 321, ind=E80), ap("nMx", 0, n16), AL.is_equal)
-        tt(ap("st2", 0, n16), ap("val0", 0, n16), ap("s80", 80 * t, 80 * t + n16), AL.add)
+        tt(ap("val0", 0, 40), ap("Vr", 0, 40), ap("nMx", 0, 40), AL.is_equal)
+        tt(ap("val0", 40, 80), ap("val0", 0, 40), ap("s80", 48 * t, 48 * t + 40), AL.add)
+        act(ap("st2", 0, n16), ap("val0", 40, 80, ind=ap("tabs", 16, 16 + nb)), AF.Identity, -400.0)
         tt(ap("val", 0, n16), ap("PS", 0, 321, ind=E80), ap("st2", 0, n16), AL.max)
+        if near[t]:
+            ql, sl = "ql%d" % t, "sl%d" % t
+            send(t, ap(qx, cast=dt.uint8), ap(ql, cast=dt.uint8), 3000 if t else 4500)
+            send(t, ap(sx), ap(sl), 2800 if t else 4200)
+            for b in range(4):
+                e = (128 * b, 128 * b + 128)
+                mm(ap("pC%d" % b, 0, C), ap("qe", *e), ap("se", *e), ap(ql), ap(sl))
+                act(ap("DW", b, 1280, 4), ap("pC%d" % b, 0, C), AF.Copy)
+                ops[-1]["rd"] += [ap("ab", 0, 1), ap("st2", 0, 1)]
         scan(ap("Fs", 0, 41 * nb), ap("fl", 0, 41 * nb), ap("ab", 0, 41 * nb), 0.0, AL.mult, AL.add)
         tt(ap("sm5", 120, 120 + nb), ap("Fs", 40, 41 * nb, 41), ap("sm5", 112, 112 + nb), AL.subtract)
         RT = ap("tabs", 40, 40 + nb)
         cp(RT, ap("sm5", 120, 120 + nb))
         cp(ap("erow", ind=RT), ap("val", 0, n16))
-        tt(ap("y2", 0, nj), ap("erow", 0, nj), ap("D4", 0, nj), AL.mult)
+        tt(ap("y2", 0, nj), ap("erow", 0, nj), ap("D4b", 0, nj), AL.mult)
         scan(ap("z2", 0, nj), ap("K4", 0, nj), ap("y2", 0, nj), 0.0, AL.mult, AL.add)
         ts(LA, ap("z2", 3, nj, 4), 4.0, AL.mult, cf(C16), AL.add)
         A = ap("At", 0, 4 * nj)
         if near[t]:
             LB = ap("LB%d" % t, 0, nj // 4)
-            send(t, LA, LB, 1800)
+            send(t, LA, LB, 2000)
             act(A, ap(X, 0, 1288, ind=LA), AF.Copy)
             lin(ap("Ah", 0, 4 * nj), A, 0.5)
             tt(ap("Mt", 0, 4 * nj), ap("DW", ind=LB), ap("Ah", 0, 4 * nj), AL.add)
@@ -457,8 +459,8 @@ def build(near):
             cp(ap("At", 0, 16 * hl), ap(X, 0, 1288, ind=ap(LA[0], 0, hl)))
             act(ap("At", 16 * hl, 4 * nj), ap(X, 0, 1288, ind=ap(LA[0], hl, nj // 4)), AF.Copy)
             quant(ap("qa"), ap("sa"), ap("At"))
-            send(t, ap("qa", 0, nj, cast=dt.uint8), ap("ql2", 80 - nj, 80, cast=dt.uint8), 3000)
-            send(t, ap("sa", 0, nj), ap("sl2", 80 - nj, 80), 2800)
+            send(t, ap("qa", 0, nj, cast=dt.uint8), ap("ql2", 80 - nj, 80, cast=dt.uint8), 3400)
+            send(t, ap("sa", 0, nj), ap("sl2", 80 - nj, 80), 3200)
             lin(ap("Ah", 0, 4 * nj), A, 0.5)
             for b in range(4):
                 e = (128 * b, 128 * b + 128)
@@ -472,8 +474,8 @@ def build(near):
             for s in range(2):
                 o = 1288 + 160 * s + b
                 tt(ap(X, o, o + 2 * nj - 3, 4), ap("Rr", 80 * b + s, 80 * b + nj, 2), ap("At", 4 * s + b, 4 * nj, 8), AL.add)
-        tt(ap("val0"), ap("val", 0, 80), ap("D16"), AL.mult)
-        scan(ap("T3", 0, 80), m16(80, "KP"), ap("val0"), 0.0, AL.mult, AL.add)
+        tt(ap("ZC", 0, n16), ap("val", 0, n16), ap("D16", 0, n16), AL.mult)
+        scan(ap("T3", 0, n16), m16(n16, "KP"), ap("ZC", 0, n16), 0.0, AL.mult, AL.add)
         tr(ap("T1"), ap("T3"))
         if t < 2:
             lin(ap("T2"), ap("T1", ind=SW), -1.0)
@@ -492,30 +494,33 @@ def build(near):
         QT = ap("tabs", 46, 46 + nb)
         ts(QT, sb(4), cf(QO), AL.add)
         cp(ap(W, 800, 2400, ind=QT), ap("vm", 80 * t, 80 * t + n16))
-        scan(ap("nr"), ap(W, 800, 1120), ap(W, 1600, 1920), 0.0, AL.max, AL.max)
+        scan(ap("io4"), ap(W, 800, 1120), ap(W, 1600, 1920), 0.0, AL.max, AL.max)
         for h in range(4):
             if h % 2 or t < 2:
-                lin(ap("ym", h, 320, 4), ap("nr", h, 320, 4), cf(MH + h))
+                lin(ap("ym", h, 320, 4), ap("io4", h, 320, 4), cf(MH + h))
             else:
-                ts(ap("ym", h, 320, 4), ap("nr", h, 320, 4), cf(MH + h), AL.mult)
+                ts(ap("ym", h, 320, 4), ap("io4", h, 320, 4), cf(MH + h), AL.mult)
         scan(ap("L2"), ap("K4"), ap("ym"), 0.0, AL.mult, AL.add)
         tt(ap("li"), ap("L2", 3, 320, 4), ap("x80"), AL.add)
         ts(ap("lj"), ap("li"), 4095, AL.bitwise_and)
         cp(ap("LX"), ap("lj"))
         xv = XS[t]
         cp(ap(Xn, 0, 16 * xv), ap(X, ind=ap("LX", 0, xv)))
-        act(ap(Xn, 16 * xv, 1280), ap(X, ind=ap("LX", xv, 80)), AF.Copy)
+        if xv < 40:
+            act(ap(Xn, 16 * xv, 640), ap(X, ind=ap("LX", xv, 40)), AF.Copy)
+        act(ap(Xn, 640, 1280), ap(X, ind=ap("LX", 40, 80)), AF.Copy)
 
     for k in range(2):
         c = (160 * k, 160 * k + 160)
         quant(ap("qx3", *c), ap("sx3", *c), ap("XW1", 4 * c[0], 4 * c[1]))
         mm(ap("pA" if k else "pB", 0, 160), ap("qv"), ap("sv"), ap("qx3", *c), ap("sx3", *c))
+        dma("Y", "oc%d" % k, [], [ap("qx3", *c)])
     act(ap("SP", 0, 160), ap("pB", 0, 160), AF.Copy)
     cp(ap("SP", 160, 320), ap("pA", 0, 160))
-    dma("S", "oc", [], [ap("qx3")])
     for k in range(4):
-        dma("YS"[k % 2], "os%d" % k, [], [ap("sx3")])
-    dma("Y", "y", [], [ap("SP")])
+        dma("YS"[k % 2], "os%d" % k, [], [ap("sx3")], 1800)
+    dma("S", "y0", [], [ap("SP", 0, 160)])
+    dma("S", "y1", [], [ap("SP", 160, 320)])
     dma("Y", "oz", [], [nn(3, 40)])
     first(20000.0)
     return ops
@@ -542,7 +547,7 @@ def depends(ops):
                     deps[k].add(j)
         for a in o["wr"]:
             for j, b, w in seen.get(a[0], []):
-                if meets(a, b):
+                if meets(a, b) and (w or ops[j]["kind"] != "dma"):
                     deps[k].add(j)
         for a in o["rd"]:
             seen.setdefault(a[0], []).append((k, a, False))
@@ -557,12 +562,29 @@ def depends(ops):
     return deps, [tail[k] + ops[k]["up"] for k in range(n)]
 
 
-def arrange(ops, deps, tail):
-    n = len(ops)
-    users = [[] for k in range(n)]
-    for k in range(n):
-        for j in deps[k]:
+def followers(deps):
+    users = [[] for d in deps]
+    for k, d in enumerate(deps):
+        for j in d:
             users[j].append(k)
+    return users
+
+
+def replay(ops, deps, seq, slow, hop):
+    free, done = {}, {}
+    for k in seq:
+        o = ops[k]
+        s = 0.0 if o["q"] == "R" else free.get(o["q"], 0.0)
+        for j in deps[k]:
+            if done[j] + hop > s:
+                s = done[j] + hop
+        free[o["q"]] = s + o["ns"]
+        done[k] = s + o["ns"] + slow * o["lat"]
+    return max(done.values())
+
+
+def arrange(ops, deps, users, tail):
+    n = len(ops)
     miss = [len(d) for d in deps]
     ready = [0.0] * n
     cand, free, seq, at, end = {}, {}, [], [0.0] * n, 0.0
@@ -597,12 +619,52 @@ def arrange(ops, deps, tail):
             miss[j] -= 1
             if not miss[j]:
                 cand.setdefault(ops[j]["q"], []).append(j)
-    return end, seq, at
+    return end + replay(ops, deps, seq, 1.4, 140.0), seq, at
+
+
+def backwards(ops, deps, users, w):
+    n = len(ops)
+    miss = [len(u) for u in users]
+    ready = [o["lat"] for o in ops]
+    cand, free, fin = {}, {}, [0.0] * n
+    for k in range(n):
+        if not miss[k]:
+            cand.setdefault(ops[k]["q"], []).append(k)
+    for i in range(n):
+        best = None
+        for q, c in cand.items():
+            if not c:
+                continue
+            now = 0.0 if q == "R" else free.get(q, 0.0)
+            now = max(now, min(ready[k] for k in c))
+            go = max((k for k in c if ready[k] <= now), key=lambda k: (w[k], k))
+            if best is None or now < best[0]:
+                best = (now, go)
+        s, k = best
+        cand[ops[k]["q"]].remove(k)
+        fin[k] = s + ops[k]["ns"]
+        free[ops[k]["q"]] = fin[k]
+        for j in deps[k]:
+            ready[j] = max(ready[j], fin[k] + HOP + ops[j]["lat"])
+            miss[j] -= 1
+            if not miss[j]:
+                cand.setdefault(ops[j]["q"], []).append(j)
+    return fin
 
 
 def order(ops):
     deps, tail = depends(ops)
-    best = arrange(ops, deps, tail)
+    users = followers(deps)
+    best = arrange(ops, deps, users, tail)
+    got = best
+    for i in range(6):
+        other = backwards(ops, deps, users, [got[2][k] + o["ns"] + o["lat"] for k, o in enumerate(ops)])
+        for k, o in enumerate(ops):
+            if o["kind"] == "dma":
+                other[k] += o["up"]
+        got = arrange(ops, deps, users, other)
+        if got[0] < best[0]:
+            best, tail = got, other
     r = [12345]
 
     def draw(m):
@@ -610,9 +672,9 @@ def order(ops):
         return (r[0] >> 8) % m
     for i in range(TRIES):
         other = list(tail)
-        for j in range(1 << draw(4)):
-            other[draw(len(ops))] += (200.0, 600.0, 1500.0, 4000.0)[draw(4)] * (1 - 2 * draw(2))
-        got = arrange(ops, deps, other)
+        for j in range(1 << draw(3)):
+            other[draw(len(ops))] += (100.0, 300.0, 800.0, 2000.0)[draw(4)] * (1 - 2 * draw(2))
+        got = arrange(ops, deps, users, other)
         if got[0] <= best[0]:
             best, tail = got, other
     for k, o in enumerate(ops):
@@ -687,9 +749,12 @@ def rank_program(g, core, T, topo):
 
     u8 = dt.uint8
     sides = {"pq": (T.ql2[:, 80:208].bitcast(u8), T.qx0[:, 0:128].bitcast(u8)), "ps": (T.sl2[:, 80:208], T.sx0[:, 0:128]),
-             "x": (T.XW0[:, 0:1280], T.x[:]), "u": (T.ut[:], T.u[:]), "v": (T.vt[:], T.v[:]), "z": (T.zi[:], T.z[:]),
-             "wc": (T.qw[:].bitcast(u8), T.wc[:]), "ws": (T.sw[:], T.ws[:]), "y": (T.y[:], T.SP[:]),
-             "oc": (T.oc[:], T.qx3[:].bitcast(u8)), "oz": (T.oz[:], T.NN[0:128:16, 144:184])}
+             "u": (T.ut[:], T.u[:]), "v": (T.vt[:], T.v[:]), "z": (T.zi[:], T.z[:]),
+             "wc": (T.qw[:].bitcast(u8), T.wc[:]), "ws": (T.sw[:], T.ws[:]), "oz": (T.oz[:], T.NN[0:128:16, 144:184])}
+    for m in range(2):
+        sides["x%d" % m] = (T.XW0[:, 640 * m:640 * m + 640], T.x[:, 640 * m:640 * m + 640])
+        sides["y%d" % m] = (T.y[:, 160 * m:160 * m + 160], T.SP[:, 160 * m:160 * m + 160])
+        sides["oc%d" % m] = (T.oc[:, 640 * m:640 * m + 640], T.qx3[:, 160 * m:160 * m + 160].bitcast(u8))
     for m in range(4):
         sides["os%d" % m] = (T.osc[4 * m:4 * m + 4, :], T.sx3[32 * m:32 * m + 4, :])
     calls = {"affine_select": g.affine_select, "matmul_mx": g.tensor.matmul_mx, "tensor_tensor": g.vector.tensor_tensor,
@@ -736,5 +801,5 @@ def rank_program(g, core, T, topo):
         if k in num:
             i.then_inc(T.sem["e" + o["q"]], 1)
     g.wait_ge(T.sem.sent, sent)
-    for k in DMAS[8:]:
+    for k in DMAS[9:]:
         g.sync.wait_ge(T.sem["d" + k], 16)

from concourse.mybir import dt, AluOpType, ActivationFunctionType

C = 320
NJ = [64, 72, 72]
NB = [4, 5, 5]
STEP = [1, 2, 4]
XS = [32, 36, 40]
F32, BF, I32, U16, Q8, U8 = "float32", "bfloat16", "int32", "uint16", "float8_e4m3fn_x4", "uint8"
BIG = 1e29
HOP = 90.0
TRIES = 3500

SCRATCH = {}


def _decl(names, n, d, where="sbuf"):
    for k in names.split():
        SCRATCH[k] = (where, [128, n], d)


_decl("XW0 XW1", 1608, BF)
_decl("DW", 1288, BF)
_decl("ut vt At Mt", 512, BF)
_decl("Ah", 320, BF)
_decl("Eb", 516, BF)
_decl("qx0 qx1 qx2 qx3 ql0 ql1", 320, Q8)
_decl("sx0 sx1 sx2 sx3 sl0 sl1", 320, U8)
_decl("ql2", 208, Q8)
_decl("sl2", 208, U8)
_decl("qw qe", 512, Q8)
_decl("sw se", 512, U8)
_decl("qu qp qv qa qm", 128, Q8)
_decl("su sp sv sa sm", 128, U8)
_decl("pA pB pD pE pC0 pC1 pC2 pC3", 512, F32, "psum")
_decl("SP nr cm K4 io4 ym L2 Rr", 320, F32)
_decl("M Mx PS", 336, F32)
_decl("WZ", 3200, F32)
_decl("R0", 768, F32)
_decl("LA0 LA1 LA2 LB0 LB1", 20, U16)
_decl("LX tabs tz", 80, U16)
_decl("zi pI", 2, I32)
_decl("CI", 8, I32)
_decl("CF", 32, F32)
_decl("zb zT", 64, F32)
_decl("MK KP io", 384, F32)
_decl("D16 D4 D4b lev ctab nMx st2 val0 erow y2 z2 g80 x80", 80, F32)
_decl("val T1 T2 T3 vb uu ww src V1", 96, F32)
_decl("tb ab fl Fs io3", 208, BF)
_decl("kk Vr yv Vo", 48, F32)
_decl("NN va tr jk V0 g2 o2", 192, F32)
_decl("ES", 384, F32)
_decl("s80 vm vs", 240, F32)
_decl("ZM ZO", 288, F32)
_decl("ZA ZB ZC SR sm5", 128, F32)
_decl("ow", 256, F32)
_decl("li lj", 80, I32)

DMAS = ["pq", "ps", "x0", "x1", "u", "z", "wc", "ws", "v", "y0", "y1", "oc0", "oc1", "oz", "os0", "os1", "os2", "os3"]
SEMAPHORES = ["eV", "eS", "eP", "eG", "sent"] + ["d" + k for k in DMAS] + ["r%d" % k for k in range(8)]


def ap(name, lo=0, hi=None, step=1, ind=None, cast=None):
    if hi is None:
        hi = SCRATCH[name][1][1]
    return (name, lo, hi, step, ind, cast)


def col(name, c):
    return ap(name, c, c + 1)


def count(a):
    if a[4] is not None:
        return 16 * (a[4][2] - a[4][1])
    return len(range(a[1], a[2], a[3]))


def build(near):
    ops = []
    AL, AF = AluOpType, ActivationFunctionType

    def two(a):
        return SCRATCH[a[0]][2] in (BF, U16)

    def rec(q, kind, args, outs, ins, ns, lat=0):
        rd, wr = [], []
        for a in ins:
            if isinstance(a, tuple):
                (wr if SCRATCH[a[0]][0] == "psum" else rd).append(a)
                if a[4] is not None:
                    rd.append(a[4])
        for a in outs:
            wr.append(a)
            if a[4] is not None:
                rd.append(a[4])
        ops.append({"q": q, "kind": kind, "args": args, "rd": rd, "wr": wr, "ns": ns, "lat": lat, "up": 0.0})
        return len(ops) - 1

    def first(v=1500.0):
        ops[-1]["up"] = v

    def vns(out, a, k=1.0):
        if out[4] is not None:
            return 60 + 3.8 * count(out)
        if a[4] is not None:
            return 60 + 1.6 * count(a)
        return max(64, k * count(out)) + 10

    def half(*aps):
        return 0.5 if all(two(a) for a in aps) else 1.0

    def tt(out, a, b, op):
        k = 1.0 if "psum" in (SCRATCH[a[0]][0], SCRATCH[b[0]][0]) else 2.0
        rec("V", "tensor_tensor", (out, a, b, op), [out], [a, b], vns(out, a, k))

    def ts(out, a, s1, op0, s2=None, op1=None):
        args = (out, a, s1, s2, op0) if op1 is None else (out, a, s1, s2, op0, op1)
        rec("V", "tensor_scalar", args, [out], [a, s1, s2], vns(out, a, half(out, a)))

    def cp(out, a):
        rec("V", "tensor_copy", (out, a), [out], [a], vns(out, a, half(out, a)))

    def scan(out, a, b, init, op0, op1):
        rec("V", "tensor_tensor_scan", (out, a, b, init, op0, op1), [out], [a, b, init], vns(out, a, half(out, a, b)))

    def mset(out, v):
        rec("V", "memset", (out, v), [out], [], vns(out, out, half(out)))

    def tr(out, a):
        rec("V", "transpose", (out, a), [out], [a], vns(out, a))

    def quant(q, s, a):
        rec("V", "quantize_mx", (q, s, a), [q, s], [a], 20 + 0.27 * count(a))

    def act(out, a, f, bias=None, scale=None, acc=None):
        n = 95 + (1.6 if a[4] is not None else 1.0) * count(a) + (25 if acc else 0)
        rec("S", "activation", (out, a, f, bias, scale, acc), [out] + ([acc] if acc else []), [a, bias, scale], n)

    def lin(out, a, scale, bias=None):
        act(out, a, AF.Identity, bias, scale)

    def mm(out, w, ws, x, xs):
        rec("P", "matmul_mx", (out, w, ws, x, xs, True, True), [ap(out[0])], [w, ws, x, xs], 20 + 0.8 * count(x))

    def iota(out, pat, base, ch=0):
        rec("G", "iota", (out, pat, base, ch), [out], [], 130 + 2.0 * count(out))

    def fill(out, v=0):
        iota(out, [[0, count(out)]], v)

    def dma(q, name, outs, ins, lat=2000):
        rec(q, "dma", name, outs, ins, 80, lat)

    rn = [0]

    def send(t, src, dst, lat):
        k = rec("G", "send", (t, src, dst, rn[0]), [], [src], 300)
        j = rec("R", "recv", (t, rn[0]), [dst], [], 0, lat)
        ops[j]["after"] = k
        rn[0] += 1

    dma("S", "z", [ap("zi")], [])
    first(90000.0)
    dma("Y", "x0", [ap("XW0", 0, 640)], [], 2300)
    first(95000.0)
    dma("Y", "x1", [ap("XW0", 640, 1280)], [], 2700)
    first(90000.0)
    dma("S", "u", [ap("ut")], [], 2300)
    first(80000.0)
    dma("Y", "wc", [ap("qw")], [ap("XW0", 1272, 1280)], 3500)
    first(30000.0)
    dma("Y", "ws", [ap("sw")], [ap("XW0", 1272, 1280)], 3500)
    first(30000.0)
    dma("Y", "v", [ap("vt")], [ap("qw")], 3500)
    first(40000.0)

    P3, SG, H8, P16, P32, H, I8, X4, SIG, NSG, BGB, THR, C16, RZB, QO, SO, I2, N4, MH = range(19)
    iota(col("pI", 0), [[0, 1]], 0, 1)
    first(9000.0)
    p = col("pI", 0)
    ts(col("CI", P3), p, 3, AL.bitwise_and)
    ts(col("CI", SG), p, 2, AL.logical_shift_right, 1, AL.bitwise_and)
    ts(col("CI", H8), p, 3, AL.logical_shift_right, 1, AL.bitwise_and)
    ts(col("CI", P16), p, 15, AL.bitwise_and)
    ts(col("CI", P32), p, 31, AL.bitwise_and)
    ts(col("CI", H), p, 2, AL.logical_shift_right, 3, AL.bitwise_and)
    cp(ap("CF", 0, 6), ap("CI", 0, 6))

    def cf(k):
        return col("CF", k)
    lin(cf(I8), cf(H8), 4.0, cf(P3))
    lin(cf(X4), cf(SG), -8.0, cf(P16))
    lin(cf(SIG), cf(SG), -2.0, 1.0)
    lin(cf(NSG), cf(SG), -1.0)
    ts(cf(BGB), cf(SG), -BIG, AL.mult, BIG, AL.add)
    lin(cf(THR), cf(SG), -1e26, -0.5e26)
    lin(cf(C16), cf(P3), 1.0, 1600.0)
    lin(cf(RZB), cf(SG), 64.0, 19.5)
    lin(cf(QO), cf(SG), -800.0, 800.0)
    lin(cf(SO), cf(SG), -1600.0, 1600.0)
    lin(cf(26), cf(SG), 800.0)
    lin(cf(I2), cf(I8), 2.0, cf(SG))
    lin(cf(N4), cf(SG), -1.0, 400.0)
    iota(ap("ctab"), [[16, 80]], 0)
    iota(ap("io", 0, 96), [[0, 12], [1, 8]], 0)
    iota(ap("io", 96, 192), [[0, 12], [1, 8]], 0)
    iota(ap("io", 288, 384), [[0, 6], [1, 16]], 0)
    for lo, hi, k in ((0, 96, I8), (96, 192, I8), (288, 384, P16)):
        ts(ap("MK", lo, hi), ap("io", lo, hi), cf(k), AL.is_equal)
        act(ap("KP", lo, hi), ap("io", lo, hi), AF.Sign)

    def m16(n, k="MK"):
        return ap(k, 288, 288 + n)
    lin(ap("D16"), m16(80), cf(SIG))
    for k in range(2):
        iota(ap("io4", 160 * k, 160 * k + 160), [[0, 40], [1, 4]], 0)
        iota(ap("cm", 160 * k, 160 * k + 160), [[1, 160]], 160 * k - 400)
    ts(ap("D4b"), ap("io4", 0, 80), cf(H), AL.is_equal)
    lin(ap("CF", MH, MH + 4), ap("D4b", 0, 4), 4.0)
    act(ap("K4"), ap("io4"), AF.Sign)
    iota(ap("io3", 0, 205), [[-8, 5], [1, 41]], 0)
    ts(ap("Fs", 0, 205), ap("io3", 0, 205), cf(I8), AL.not_equal, 2.0, AL.mult)
    lin(ap("fl", 0, 205), ap("Fs", 0, 205), 1.0, -1.0)
    mset(ap("fl", 0, 205, 41), 0.0)
    UT, ZT, SW, DUP, DUP2 = [ap("tabs", a, b) for a, b in ((0, 8), (8, 10), (10, 16), (16, 21), (22, 27))]
    RZ, RZ2, ST0 = ap("tabs", 28, 33), ap("tabs", 34, 39), ap("tabs", 52, 56)
    cp(UT, ap("ctab", 0, 8))
    ts(ZT, ap("ctab", 0, 4, 2), cf(P32), AL.add)
    ts(SW, ap("ctab", 0, 6), cf(X4), AL.add, 4.0, AL.add)
    K6 = ap("sm5", 16, 22)
    lin(K6, ap("ctab", 0, 6), 0.5, cf(I8))
    cp(DUP, ap("sm5", 16, 21))
    lin(col("sm5", 30), cf(SG), 48.0)
    ts(DUP2, ap("sm5", 16, 21), col("sm5", 30), AL.add)
    lin(ap("tb", 40, 205, 41), ap("ctab", 0, 5), 1.0, cf(I2))
    lin(ap("ow", 200, 206), K6, 1.0, 704.0)
    lin(ap("sm5", 8, 12), ap("ow", 200, 204), cf(SG))
    lin(ap("T2", 0, 80), ap("ctab"), 1.0, cf(P16))
    lin(ap("x80"), ap("T2", 0, 80), 1.0, -1600.0)
    lin(ap("kk"), ap("ctab", 0, 48), 1.0 / 1024)
    iota(ap("lev"), [[0, 10], [1, 2], [0, 4]], 0)
    iota(ap("sm5", 32, 38), [[4, 3], [0, 2]], 17)
    iota(ap("sm5", 40, 45), [[1, 5]], 0)
    act(ap("vb", 48, 96), ap("kk"), AF.Relu, -31.0, 64.0)
    act(ap("src", 32, 48), ap("kk", 32, 48), AF.Identity, 322.0 - 40 * 32, 40 * 64.0)
    lin(ap("V0", 48, 96), ap("kk"), 0.0, -BIG)
    lin(ap("V0", 144, 192), ap("kk"), 0.0, -BIG)
    lin(ap("g80"), ap("lev"), -BIG, -1.0)
    for k in range(2):
        fill(ap("XW%d" % k, 1280, 1444))
        fill(ap("XW%d" % k, 1444, 1608))
        fill(ap("Mt", 256 + 128 * k, 384 + 128 * k))
        fill(ap("At", 256 + 128 * k, 384 + 128 * k))
    fill(ap("DW", 1280, 1288))
    for k in ("M", "Mx", "PS"):
        mset(ap(k, 0, 1), -400.0)
    fill(ap("T3", 64, 96))
    mset(ap("R0", 0, 320), 0.0)
    first(9000.0)
    fill(ap("NN", 32, 48))
    fill(ap("vb", 38, 48))
    fill(ap("vb", 32, 33), 34)
    fill(ap("SR", 40, 48))
    fill(ap("SR", 104, 112))
    mset(ap("Eb"), 0.5)
    first(20000.0)
    rec("G", "affine_select", (ap("Eb"), ap("Eb"), [[-1, 516]], AL.is_equal, 0.0, 3, 4), [ap("Eb")], [ap("Eb")], 1200)
    first(6000.0)
    for b in range(4):
        quant(ap("qe", 128 * b, 128 * b + 128), ap("se", 128 * b, 128 * b + 128), ap("Eb", 3 - b, 515 - b))
        first(5000.0)
    for lo in (0, 160, 800, 960, 1600, 1760, 2400, 2560):
        fill(ap("WZ", lo, lo + 160))

    quant(ap("qu"), ap("su"), ap("ut"))
    cp(ap("qp", cast=dt.uint32), ap("qu", ind=UT, cast=dt.uint32))
    act(ap("sp"), ap("su", ind=UT), AF.Copy)
    quant(ap("qv"), ap("sv"), ap("vt"))

    cp(ap("CF", 24, 26), ap("zi"))
    for b in range(2):
        lin(ap("zb", 32 * b, 32 * b + 32), ap("ctab", 0, 32), 0.0, cf(24 + b))
    tr(ap("zT"), ap("zb"))
    cp(ap("NN", 0, 32), ap("zT", ind=ZT))

    def nn(t, n=48):
        return ap("NN", 48 * t, 48 * t + n)

    def en(t, n=48):
        o = (0, 96, 144, 288)[t]
        return ap("ES", o, o + n)

    def st(t, n=48):
        o = (48, 192, 240, 336)[t]
        return ap("ES", o, o + n)
    scan(en(0), nn(0), nn(0), 0.0, AL.add, AL.max)
    tt(st(0), en(0), nn(0), AL.subtract)
    tt(ap("ZA", 0, 96), ap("ES", 0, 96), ap("MK", 0, 96), AL.mult)
    scan(ap("ZB", 0, 96), ap("KP", 0, 96), ap("ZA", 0, 96), 0.0, AL.mult, AL.add)
    tt(ap("sm5", 48, 52), ap("ZB", 55, 87, 8), ap("sm5", 8, 12), AL.max)
    cp(ST0, ap("sm5", 48, 52))
    mset(ap("jk", 0, 64), -BIG)
    cp(ap("R0", ind=ST0), ap("jk", 0, 64))
    cp(ap("tz", 0, 6), ap("ZB", 7, 48, 8))
    tt(ap("g2", 0, 48), en(0), m16(48), AL.mult)
    scan(ap("o2", 0, 48), m16(48, "KP"), ap("g2", 0, 48), 0.0, AL.mult, AL.add)
    cp(ap("tz", 20, 23), ap("o2", 15, 48, 16))

    def giving(t):
        lo, hi = 48 * t, 48 * t + 48
        lin(ap("va", lo, hi), ap("NN", lo, hi), 1e26, cf(THR))
        ts(ap("tr", lo, hi), ap("va", lo, hi), -1.0, AL.mult, 320.0, AL.min)
        tt(ap("s80", lo, hi), ap("tr", lo, hi), st(t), AL.max)
    giving(0)

    act(ap("vb", 0, 32), nn(0, 32), AF.Copy)
    for j in range(5):
        act(ap("ZM", 32 * j, 32 * j + 32), nn(0, 32), AF.Sign, -1.5 - j, None, col("sm5", 56 + j))
    lin(col("sm5", 62), col("sm5", 56), 0.5, 16.0)
    ts(ap("sm5", 64, 69), ap("sm5", 40, 45), col("sm5", 62), AL.is_le)
    lin(ap("sm5", 88, 93), ap("sm5", 56, 61), 0.5)
    tt(ap("sm5", 96, 101), ap("sm5", 88, 93), ap("sm5", 33, 38), AL.add)
    tt(ap("vb", 33, 38), ap("sm5", 96, 101), ap("sm5", 64, 69), AL.add)
    tt(ap("ZC", 64, 104), ap("vb", 0, 40), ap("kk", 0, 40), AL.subtract)
    tt(ap("ZC", 0, 40), ap("ZC", 64, 104), ap("MK", 0, 40), AL.mult)
    scan(ap("ZA", 40, 80), ap("KP", 0, 40), ap("ZC", 0, 40), 0.0, AL.mult, AL.add)
    for m in range(5):
        act(ap("ZO", 40 * m, 40 * m + 40), ap("ZC", 64, 104), AF.Sign, col("ZA", 47 + 8 * m), -1.0, col("sm5", 104 + m))
    ts(RZ, ap("sm5", 104, 109), -0.5, AL.mult, cf(RZB), AL.add)
    ts(RZ2, ap("sm5", 104, 109), -0.5, AL.mult, 19.5, AL.add)
    act(ap("D4"), ap("vb", ind=DUP2), AF.Copy)
    cp(ap("SR", ind=RZ), ap("D4"))
    for t in (1, 2):
        u = ap("uu", 48 * t - 48, 48 * t)
        w = ap("ww", 48 * t - 48, 48 * t)
        act(u, ap("SR", 64, 112), AF.Relu, -2000.0 * t, 1000.0)
        tt(w, ap("SR", 0, 48), u, AL.subtract)
        act(nn(t), w, AF.Relu, -2.0 * t)
    act(nn(3), ap("SR", 0, 48), AF.Relu, -6.0)
    for t in (1, 2, 3):
        scan(en(t), nn(t), nn(t), 0.0, AL.add, AL.max)
        tt(st(t), en(t), nn(t), AL.subtract)
    giving(1)
    giving(2)
    tt(ap("io", 0, 192), ap("ES", 96, 288), ap("MK", 0, 192), AL.mult)
    scan(ap("ZO", 0, 192), ap("KP", 0, 192), ap("io", 0, 192), 0.0, AL.mult, AL.add)
    tt(ap("io", 192, 288), ap("ES", 288, 384), ap("MK", 0, 96), AL.mult)
    scan(ap("ZO", 192, 288), ap("KP", 0, 96), ap("io", 192, 288), 0.0, AL.mult, AL.add)
    cp(ap("tz", 6, 18), ap("ZO", 7, 96, 8))
    tt(ap("jk", 0, 96), ap("ES", 96, 192), m16(96), AL.mult)
    scan(ap("jk", 96, 192), m16(96, "KP"), ap("jk", 0, 96), 0.0, AL.mult, AL.add)
    cp(ap("tz", 24, 27), ap("jk", 111, 144, 16))
    cp(ap("tz", 28, 31), ap("jk", 159, 192, 16))
    act(ap("src", 0, 32), st(0, 32), AF.Copy)
    lin(ap("src", 48, 96), ap("src", 0, 48), 1.0, 1.0)
    act(ap("z2"), ap("src", ind=DUP2), AF.Identity, 401.0)
    act(ap("T1", 0, 80), ap("ES", 192, 240, ind=RZ2), AF.Identity, None, 1023.0)
    tt(ap("vm", 0, 80), ap("T1", 0, 80), ap("z2"), AL.add)
    tt(ap("vs", 0, 80), ap("vm", 0, 80), ap("g80"), AL.add)
    lin(ap("ww"), ap("uu"), 0.04, 282.0)
    tt(ap("ZM", 0, 96), ap("ww"), ap("uu"), AL.min)
    tt(ap("ww"), ap("ZM", 0, 96), ap("ES", 192, 288), AL.max)
    for t in (1, 2):
        lin(ap("uu", 48 * t - 48, 48 * t), st(t + 1), 1023.0, 400.0 + 524288.0 * t)
        v0 = ap("V0", 96 * t - 96, 96 * t - 48)
        tt(v0, ap("uu", 48 * t - 48, 48 * t), ap("ww", 48 * t - 48, 48 * t), AL.add)
        for k in range(2):
            lin(ap("V1", 48 * k, 48 * k + 48), v0, 1.0, 1.0 + k)
        act(ap("vm", 80 * t, 80 * t + 80), ap("V1", ind=DUP2), AF.Copy)
        act(ap("vs", 80 * t, 80 * t + 80), ap("V0", v0[1], v0[1] + 96, ind=DUP2), AF.Copy)
    tt(ap("g2", 0, 80), ap("ES", 96, 144, ind=RZ2), m16(80), AL.mult)
    tt(ap("g2", 96, 176), ap("ES", 192, 240, ind=RZ2), m16(80), AL.mult)
    scan(ap("o2", 0, 80), m16(80, "KP"), ap("g2", 0, 80), 0.0, AL.mult, AL.add)
    scan(ap("o2", 96, 176), m16(80, "KP"), ap("g2", 96, 176), 0.0, AL.mult, AL.add)

    def ow(k, t, n=5):
        return ap("ow", 20 * k + 6 * t, 20 * k + 6 * t + n)

    def moves(t, e0, s0, e1, s1):
        tt(ow(4, t), e0, s0, AL.subtract)
        ts(ow(5, t), ow(4, t), 2.0, AL.is_le, 800.0, AL.mult)
        tt(ow(6, t), e1, ow(5, t), AL.subtract)
        tt(ow(7, t), s1, s0, AL.subtract)
        tt(ow(8, t), e1, s1, AL.is_equal)
        tt(ow(9, t), ow(8, t), ow(10, 0), AL.mult)
        tt(ow(3, t), ow(9, t), s1, AL.max)
        ts(ap("tz", 40 + 6 * t, 45 + 6 * t), ow(3, t), cf(26) if t == 1 else cf(SO), AL.add)

    def zo(o):
        return ap("ZO", o + 7, o + 47, 8)
    moves(0, ap("ZB", 7, 47, 8), ap("ZB", 55, 95, 8), ap("o2", 15, 80, 16), ap("o2", 111, 176, 16))
    moves(1, zo(0), zo(96), zo(48), zo(144))
    moves(2, zo(48), zo(144), zo(192), zo(240))

    for t in range(3):
        nj, nb = NJ[t], NB[t]
        n16 = 16 * nb
        E80, E48 = ap("tz", 6 * t, 6 * t + nb), ap("tz", 20 + 4 * t, 23 + 4 * t)
        X, Xn, W = "XW%d" % (t % 2), "XW%d" % (1 - t % 2), "WZ"
        qx, sx, LA = "qx%d" % t, "sx%d" % t, ap("LA%d" % t, 0, nj // 4)
        R = [ap("R0", 0, 320), ap(W, 0, 320), ap(W, 2400, 2720)][t]
        lo, hi = (1600, 3200) if t == 1 else (0, 2400)
        cp(ap(W, lo, hi, ind=ap("tz", 40 + 6 * t, 45 + 6 * t)), ap("vs", 80 * t, 80 * t + 80))
        first(3000.0 if t else 0.0)
        for c0, c1, b0, b1 in ((0, 160, "pA", "pB"), (160, C, "pD", "pE")):
            quant(ap(qx, c0, c1), ap(sx, c0, c1), ap(X, 4 * c0, 4 * c1))
            for b in (b0, b1):
                mm(ap(b, 0, c1 - c0), ap("qp"), ap("sp"), ap(qx, c0, c1), ap(sx, c0, c1))
            lin(ap("SP", c0, c1), ap(b0, 0, c1 - c0), cf(SIG))
            r = ap(R[0], R[1] + c0, R[1] + c1)
            scan(ap("Mx", 1 + c0, 1 + c1), r, ap(b1, 0, c1 - c0), col("Mx", c0), AL.add, AL.max)
            scan(ap("M", 1 + c0, 1 + c1), r, ap("SP", c0, c1), col("M", c0), AL.add, AL.max)
            tt(ap("nr", c0, c1), ap("M", 1 + c0, 1 + c1), ap("M", c0, c1), AL.is_equal)
        scan(ap("PS", 1, 321), ap("nr"), ap("cm"), 0.0, AL.mult, AL.min)
        if t == 1:
            dma("Y", "pq", [ap("ql2", 80, 208)], [ap("qx0"), ap("PS")])
            dma("Y", "ps", [ap("sl2", 80, 208)], [ap("sx0"), ap("PS")])
        tt(ap("Vr"), ap("M", 0, 321, ind=E48), ap("va", 48 * t, 48 * t + 48), AL.min)
        first()
        tt(ap("yv", 0, 8 * nb), ap("Vr", 0, 8 * nb), ap("MK", 0, 8 * nb), AL.mult)
        first()
        scan(ap("Vo", 0, 8 * nb), ap("KP", 0, 8 * nb), ap("yv", 0, 8 * nb), 0.0, AL.mult, AL.add)
        first()
        act(ap("nMx", 0, 48), ap("Mx", 0, 321, ind=E48), AF.Identity, cf(BGB), cf(NSG))
        first()
        for m in range(nb):
            act(ap("tb", 41 * m, 41 * m + 40), ap("Vr", 0, 40), AF.Sign, col("Vo", 8 * m + 7), -1.0, col("sm5", 112 + m))
        act(ap("ab", 0, 41 * nb), ap("tb", 0, 41 * nb), AF.Abs)
        tt(ap("val0", 0, 40), ap("Vr", 0, 40), ap("nMx", 0, 40), AL.is_equal)
        tt(ap("val0", 40, 80), ap("val0", 0, 40), ap("s80", 48 * t, 48 * t + 40), AL.add)
        act(ap("st2", 0, n16), ap("val0", 40, 80, ind=ap("tabs", 16, 16 + nb)), AF.Identity, -400.0)
        tt(ap("val", 0, n16), ap("PS", 0, 321, ind=E80), ap("st2", 0, n16), AL.max)
        if near[t]:
            ql, sl = "ql%d" % t, "sl%d" % t
            send(t, ap(qx, cast=dt.uint8), ap(ql, cast=dt.uint8), 3000 if t else 4500)
            send(t, ap(sx), ap(sl), 2800 if t else 4200)
            for b in range(4):
                e = (128 * b, 128 * b + 128)
                mm(ap("pC%d" % b, 0, C), ap("qe", *e), ap("se", *e), ap(ql), ap(sl))
                act(ap("DW", b, 1280, 4), ap("pC%d" % b, 0, C), AF.Copy)
                ops[-1]["rd"] += [ap("ab", 0, 1), ap("st2", 0, 1)]
        scan(ap("Fs", 0, 41 * nb), ap("fl", 0, 41 * nb), ap("ab", 0, 41 * nb), 0.0, AL.mult, AL.add)
        tt(ap("sm5", 120, 120 + nb), ap("Fs", 40, 41 * nb, 41), ap("sm5", 112, 112 + nb), AL.subtract)
        RT = ap("tabs", 40, 40 + nb)
        cp(RT, ap("sm5", 120, 120 + nb))
        cp(ap("erow", ind=RT), ap("val", 0, n16))
        tt(ap("y2", 0, nj), ap("erow", 0, nj), ap("D4b", 0, nj), AL.mult)
        scan(ap("z2", 0, nj), ap("K4", 0, nj), ap("y2", 0, nj), 0.0, AL.mult, AL.add)
        ts(LA, ap("z2", 3, nj, 4), 4.0, AL.mult, cf(C16), AL.add)
        A = ap("At", 0, 4 * nj)
        if near[t]:
            LB = ap("LB%d" % t, 0, nj // 4)
            send(t, LA, LB, 2000)
            act(A, ap(X, 0, 1288, ind=LA), AF.Copy)
            lin(ap("Ah", 0, 4 * nj), A, 0.5)
            tt(ap("Mt", 0, 4 * nj), ap("DW", ind=LB), ap("Ah", 0, 4 * nj), AL.add)
        else:
            hl = nj // 8 + 1
            cp(ap("At", 0, 16 * hl), ap(X, 0, 1288, ind=ap(LA[0], 0, hl)))
            act(ap("At", 16 * hl, 4 * nj), ap(X, 0, 1288, ind=ap(LA[0], hl, nj // 4)), AF.Copy)
            quant(ap("qa"), ap("sa"), ap("At"))
            send(t, ap("qa", 0, nj, cast=dt.uint8), ap("ql2", 80 - nj, 80, cast=dt.uint8), 3400)
            send(t, ap("sa", 0, nj), ap("sl2", 80 - nj, 80), 3200)
            lin(ap("Ah", 0, 4 * nj), A, 0.5)
            for b in range(4):
                e = (128 * b, 128 * b + 128)
                mm(ap("pC%d" % b, 0, 128), ap("qe", *e), ap("se", *e), ap("ql2", 80 - nj, 208 - nj), ap("sl2", 80 - nj, 208 - nj))
                tt(ap("Mt", b, 4 * nj, 4), ap("pC%d" % b, 0, nj), ap("Ah", b, 4 * nj, 4), AL.add)
        quant(ap("qm"), ap("sm"), ap("Mt"))
        for b in range(4):
            e = (128 * b, 128 * b + 128)
            mm(ap("pC%d" % b, 0, 128), ap("qw", *e), ap("sw", *e), ap("qm"), ap("sm"))
            act(ap("Rr", 80 * b, 80 * b + nj), ap("pC%d" % b, 0, nj), AF.Relu, None, 0.03125)
            for s in range(2):
                o = 1288 + 160 * s + b
                tt(ap(X, o, o + 2 * nj - 3, 4), ap("Rr", 80 * b + s, 80 * b + nj, 2), ap("At", 4 * s + b, 4 * nj, 8), AL.add)
        tt(ap("ZC", 0, n16), ap("val", 0, n16), ap("D16", 0, n16), AL.mult)
        scan(ap("T3", 0, n16), m16(n16, "KP"), ap("ZC", 0, n16), 0.0, AL.mult, AL.add)
        tr(ap("T1"), ap("T3"))
        if t < 2:
            lin(ap("T2"), ap("T1", ind=SW), -1.0)
        else:
            ts(ap("T2"), ap("T1", ind=SW), -1.0, AL.mult)
        tr(ap("T1"), ap("T2"))

        def sb(k):
            return ap("ow", 220 + 6 * k, 220 + 6 * k + nb)
        tt(sb(3), ap("T3", 15, n16, 16), ap("T1", 15, n16, 16), AL.min)
        ts(sb(4), sb(3), cf(SIG), AL.mult, cf(N4), AL.add)
        tt(sb(3), sb(4), ow(7, t, nb), AL.add)
        tt(sb(4), sb(3), ow(6, t, nb), AL.is_ge)
        tt(sb(5), sb(4), ow(10, 0, nb), AL.mult)
        tt(sb(4), sb(5), sb(3), AL.max)
        QT = ap("tabs", 46, 46 + nb)
        ts(QT, sb(4), cf(QO), AL.add)
        cp(ap(W, 800, 2400, ind=QT), ap("vm", 80 * t, 80 * t + n16))
        scan(ap("io4"), ap(W, 800, 1120), ap(W, 1600, 1920), 0.0, AL.max, AL.max)
        for h in range(4):
            if h % 2 or t < 2:
                lin(ap("ym", h, 320, 4), ap("io4", h, 320, 4), cf(MH + h))
            else:
                ts(ap("ym", h, 320, 4), ap("io4", h, 320, 4), cf(MH + h), AL.mult)
        scan(ap("L2"), ap("K4"), ap("ym"), 0.0, AL.mult, AL.add)
        tt(ap("li"), ap("L2", 3, 320, 4), ap("x80"), AL.add)
        ts(ap("lj"), ap("li"), 4095, AL.bitwise_and)
        cp(ap("LX"), ap("lj"))
        xv = XS[t]
        cp(ap(Xn, 0, 16 * xv), ap(X, ind=ap("LX", 0, xv)))
        if xv < 40:
            act(ap(Xn, 16 * xv, 640), ap(X, ind=ap("LX", xv, 40)), AF.Copy)
        act(ap(Xn, 640, 1280), ap(X, ind=ap("LX", 40, 80)), AF.Copy)

    for k in range(2):
        c = (160 * k, 160 * k + 160)
        quant(ap("qx3", *c), ap("sx3", *c), ap("XW1", 4 * c[0], 4 * c[1]))
        mm(ap("pA" if k else "pB", 0, 160), ap("qv"), ap("sv"), ap("qx3", *c), ap("sx3", *c))
        dma("Y", "oc%d" % k, [], [ap("qx3", *c)])
    act(ap("SP", 0, 160), ap("pB", 0, 160), AF.Copy)
    cp(ap("SP", 160, 320), ap("pA", 0, 160))
    for k in range(4):
        dma("YS"[k % 2], "os%d" % k, [], [ap("sx3")], 1800)
    dma("S", "y0", [], [ap("SP", 0, 160)])
    dma("S", "y1", [], [ap("SP", 160, 320)])
    dma("Y", "oz", [], [nn(3, 40)])
    first(20000.0)
    return ops


def meets(a, b):
    if a[0] != b[0] or a[1] >= b[2] or b[1] >= a[2]:
        return False
    if a[3] == b[3] and a[3] > 1 and a[4] is None and b[4] is None:
        return (a[1] - b[1]) % a[3] == 0
    return True


def depends(ops):
    n = len(ops)
    deps = [set() for k in range(n)]
    seen = {}
    for k, o in enumerate(ops):
        if "after" in o:
            deps[k].add(o["after"])
        for a in o["rd"]:
            for j, b, w in seen.get(a[0], []):
                if w and meets(a, b):
                    deps[k].add(j)
        for a in o["wr"]:
            for j, b, w in seen.get(a[0], []):
                if meets(a, b) and (w or ops[j]["kind"] != "dma"):
                    deps[k].add(j)
        for a in o["rd"]:
            seen.setdefault(a[0], []).append((k, a, False))
        for a in o["wr"]:
            seen.setdefault(a[0], []).append((k, a, True))
        deps[k].discard(k)
    tail = [0.0] * n
    for k in range(n - 1, -1, -1):
        tail[k] += ops[k]["ns"] + ops[k]["lat"] + HOP
        for j in deps[k]:
            tail[j] = max(tail[j], tail[k])
    return deps, [tail[k] + ops[k]["up"] for k in range(n)]


def followers(deps):
    users = [[] for d in deps]
    for k, d in enumerate(deps):
        for j in d:
            users[j].append(k)
    return users


def replay(ops, deps, seq, slow, hop):
    free, done = {}, {}
    for k in seq:
        o = ops[k]
        s = 0.0 if o["q"] == "R" else free.get(o["q"], 0.0)
        for j in deps[k]:
            if done[j] + hop > s:
                s = done[j] + hop
        free[o["q"]] = s + o["ns"]
        done[k] = s + o["ns"] + slow * o["lat"]
    return max(done.values())


def arrange(ops, deps, users, tail):
    n = len(ops)
    miss = [len(d) for d in deps]
    ready = [0.0] * n
    cand, free, seq, at, end = {}, {}, [], [0.0] * n, 0.0
    for k in range(n):
        if not miss[k]:
            cand.setdefault(ops[k]["q"], []).append(k)
    while len(seq) < n:
        best = None
        for q, c in cand.items():
            if not c:
                continue
            now = 0.0 if q == "R" else free.get(q, 0.0)
            now = max(now, min(ready[k] for k in c))
            go = max((k for k in c if ready[k] <= now), key=lambda k: (tail[k], -k))
            ns = ops[go]["ns"]
            late = [k for k in c if now < ready[k] < now + ns and tail[k] - tail[go] > ns + 2 * (ready[k] - now)]
            if late:
                go = min(late, key=lambda k: (ready[k], k))
            s = max(now, ready[go])
            if best is None or s < best[0]:
                best = (s, go)
        s, k = best
        o = ops[k]
        cand[o["q"]].remove(k)
        free[o["q"]] = s + o["ns"]
        done = s + o["ns"] + o["lat"]
        end = max(end, done)
        at[k] = s
        seq.append(k)
        for j in users[k]:
            ready[j] = max(ready[j], done + HOP)
            miss[j] -= 1
            if not miss[j]:
                cand.setdefault(ops[j]["q"], []).append(j)
    return end + replay(ops, deps, seq, 1.4, 140.0), seq, at


def backwards(ops, deps, users, w):
    n = len(ops)
    miss = [len(u) for u in users]
    ready = [o["lat"] for o in ops]
    cand, free, fin = {}, {}, [0.0] * n
    for k in range(n):
        if not miss[k]:
            cand.setdefault(ops[k]["q"], []).append(k)
    for i in range(n):
        best = None
        for q, c in cand.items():
            if not c:
                continue
            now = 0.0 if q == "R" else free.get(q, 0.0)
            now = max(now, min(ready[k] for k in c))
            go = max((k for k in c if ready[k] <= now), key=lambda k: (w[k], k))
            if best is None or now < best[0]:
                best = (now, go)
        s, k = best
        cand[ops[k]["q"]].remove(k)
        fin[k] = s + ops[k]["ns"]
        free[ops[k]["q"]] = fin[k]
        for j in deps[k]:
            ready[j] = max(ready[j], fin[k] + HOP + ops[j]["lat"])
            miss[j] -= 1
            if not miss[j]:
                cand.setdefault(ops[j]["q"], []).append(j)
    return fin


def order(ops):
    deps, tail = depends(ops)
    users = followers(deps)
    best = arrange(ops, deps, users, tail)
    got = best
    for i in range(6):
        other = backwards(ops, deps, users, [got[2][k] + o["ns"] + o["lat"] for k, o in enumerate(ops)])
        for k, o in enumerate(ops):
            if o["kind"] == "dma":
                other[k] += o["up"]
        got = arrange(ops, deps, users, other)
        if got[0] < best[0]:
            best, tail = got, other
    r = [12345]

    def draw(m):
        r[0] = (r[0] * 1103515245 + 12345) % 2147483648
        return (r[0] >> 8) % m
    for i in range(TRIES):
        other = list(tail)
        for j in range(1 << draw(3)):
            other[draw(len(ops))] += (100.0, 300.0, 800.0, 2000.0)[draw(4)] * (1 - 2 * draw(2))
        got = arrange(ops, deps, users, other)
        if got[0] <= best[0]:
            best, tail = got, other
    for k, o in enumerate(ops):
        o["at"] = best[2][k]
    return best[1], deps


def waits(ops, seq, deps):
    place, cnt = {}, {}
    for k in seq:
        q = ops[k]["q"]
        cnt[q] = cnt.get(q, 0) + 1
        place[k] = cnt[q]
    known, clock, need = {}, {}, {}
    for k in seq:
        o = ops[k]
        if o["q"] == "R":
            clock[k] = {("one", k): 1}
            continue
        kn = known.setdefault(o["q"], {})
        need[k] = []
        for j in sorted(deps[k], key=lambda j: -ops[j]["at"]):
            single = ops[j]["kind"] in ("dma", "recv", "send")
            key, v = (("one", j), 1) if single else (ops[j]["q"], place[j])
            if kn.get(key, 0) >= v:
                continue
            need[k].append(j)
            for a, b in clock[j].items():
                kn[a] = max(kn.get(a, 0), b)
        clock[k] = dict(kn)
        if o["kind"] in ("dma", "send"):
            clock[k][("one", k)] = 1
        else:
            clock[k][o["q"]] = place[k]
    return need


PLANS = {}


def rank_program(g, core, T, topo):
    rank = T.rank_of(core)
    if rank is None:
        return
    mate = [T.cores[rank ^ s] for s in STEP]
    near = tuple(all(topo.chip(T.cores[r]) == topo.chip(T.cores[r ^ s]) for r in range(len(T.cores))) for s in STEP)
    if near not in PLANS:
        ops = build(near)
        seq, deps = order(ops)
        PLANS[near] = (ops, seq, waits(ops, seq, deps))
    ops, seq, need = PLANS[near]
    eng = {"V": g.vector, "S": g.scalar, "P": g.tensor, "G": g, "Y": g.sync}
    marked = set(j for k in need for j in need[k])
    num, cnt = {}, {}
    for k in seq:
        if k in marked and ops[k]["kind"] not in ("dma", "recv", "send"):
            cnt[ops[k]["q"]] = cnt.get(ops[k]["q"], 0) + 1
            num[k] = cnt[ops[k]["q"]]

    def view(a):
        if not isinstance(a, tuple):
            return a
        v = T[a[0]][:, a[1]:a[2]:a[3]] if a[3] > 1 else T[a[0]][:, a[1]:a[2]]
        if a[5] is not None:
            v = v.bitcast(a[5])
        if a[4] is not None:
            v = v.indirect(view(a[4]))
        return v

    def engines(t):
        return len(topo.engines(core, mate[t]))

    u8 = dt.uint8
    sides = {"pq": (T.ql2[:, 80:208].bitcast(u8), T.qx0[:, 0:128].bitcast(u8)), "ps": (T.sl2[:, 80:208], T.sx0[:, 0:128]),
             "u": (T.ut[:], T.u[:]), "v": (T.vt[:], T.v[:]), "z": (T.zi[:], T.z[:]),
             "wc": (T.qw[:].bitcast(u8), T.wc[:]), "ws": (T.sw[:], T.ws[:]), "oz": (T.oz[:], T.NN[0:128:16, 144:184])}
    for m in range(2):
        sides["x%d" % m] = (T.XW0[:, 640 * m:640 * m + 640], T.x[:, 640 * m:640 * m + 640])
        sides["y%d" % m] = (T.y[:, 160 * m:160 * m + 160], T.SP[:, 160 * m:160 * m + 160])
        sides["oc%d" % m] = (T.oc[:, 640 * m:640 * m + 640], T.qx3[:, 160 * m:160 * m + 160].bitcast(u8))
    for m in range(4):
        sides["os%d" % m] = (T.osc[4 * m:4 * m + 4, :], T.sx3[32 * m:32 * m + 4, :])
    calls = {"affine_select": g.affine_select, "matmul_mx": g.tensor.matmul_mx, "tensor_tensor": g.vector.tensor_tensor,
             "tensor_scalar": g.vector.tensor_scalar, "tensor_copy": g.vector.tensor_copy,
             "tensor_tensor_scan": g.vector.tensor_tensor_scan, "memset": g.vector.memset,
             "transpose": g.vector.transpose, "quantize_mx": g.vector.quantize_mx}
    sent = 0
    for k in seq:
        o = ops[k]
        if o["q"] == "R":
            continue
        e = eng[o["q"]]
        for j in need[k]:
            d = ops[j]
            if d["kind"] == "dma":
                e.wait_ge(T.sem["d" + d["args"]], 16)
            elif d["kind"] == "recv":
                e.wait_ge(T.sem["r%d" % d["args"][1]], engines(d["args"][0]))
            else:
                e.wait_ge(T.sem["e" + d["q"]], num[j])
        kind, a = o["kind"], o["args"]
        if kind == "dma":
            e.dma_start(*sides[a]).then_inc(T.sem["d" + a], 16)
            continue
        if kind == "send":
            rid, pid, se = topo.addr(mate[a[0]])
            g.remote_dma(view(a[2]), view(a[1]), T.sem["r%d" % a[3]], T.sem.sent, pid, rid, topo.mask(core, mate[a[0]]))
            sent += engines(a[0])
            continue
        v = [view(x) for x in a]
        if kind == "activation":
            kw = {}
            for name, x in zip(("bias", "scale", "accum_out"), v[3:]):
                if x is not None:
                    kw[name] = x
            i = e.activation(v[0], v[1], v[2], **kw)
        elif kind == "iota":
            if SCRATCH[a[0][0]][2] == I32:
                i = g.iota(*v)
            else:
                i = g.iota(*v, allow_small_or_imprecise_dtypes=True)
        else:
            i = calls[kind](*v)
        if k in num:
            i.then_inc(T.sem["e" + o["q"]], 1)
    g.wait_ge(T.sem.sent, sent)
    for k in DMAS[9:]:
        g.sync.wait_ge(T.sem["d" + k], 16)
